import numpy as np, ml_dtypes
CORES = [51,54,179,182]
N = 4
import mx_ref
BF = ml_dtypes.bfloat16
def entries(a):
    return np.ascontiguousarray(a.T).reshape(-1)
def table(e):
    return np.ascontiguousarray(np.reshape(e, (-1, 16)).T).astype(np.int32)
def f(rng, *shape):
    return mx_ref.flush((rng.standard_normal(shape, dtype=np.float32) * np.exp2(rng.integers(-2, 3, shape[:-1] + (1,)))).astype(BF))
def wide(rng, *shape, cols=0):
    v = rng.standard_normal(shape, dtype=np.float32) * np.exp2(rng.integers(-12, 13, shape)).astype(np.float32)
    if cols: v *= np.repeat(np.exp2(rng.integers(-cols, cols + 1, shape[:-2] + (1, shape[-1] // 4))) * (rng.random(shape[:-2] + (1, shape[-1] // 4)) > 0.0625), 4, axis=-1).astype(np.float32)
    return mx_ref.flush(v.astype(BF))
SH, CH, RD = 128, 64, 4
def lists(rng, same=False, apart=False, ends=False):
    a = []
    for r in range(N):
        p = rng.permutation(SH); e = []
        for t in range(1, RD):
            if same: c = p[:CH]
            elif apart: c = p[np.arange(CH * (t - 1), CH * t) % SH]
            elif ends: c = np.concatenate([[0, SH - 1], 1 + rng.permutation(SH - 2)[:CH - 2]])
            else: c = rng.permutation(SH)[:CH]
            e.append(rng.permutation(c))
        a.append(table(np.concatenate(e)))
    return {"idx": np.stack(a)}
def setup_inputs(rng):
    return {"wm": f(rng, N, 128, 4 * SH), "dl": f(rng, N, 128, (RD - 1) * 4 * CH), **lists(rng), "x": f(rng, N, 128, RD * 512)}
def setup_inputs_same(rng):
    return {**setup_inputs(rng), **lists(rng, same=True)}
def setup_inputs_apart(rng):
    return {**setup_inputs(rng), **lists(rng, apart=True)}
def setup_inputs_ends(rng):
    return {**setup_inputs(rng), **lists(rng, ends=True)}
def setup_inputs_big(rng):
    d = setup_inputs(rng); d["dl"] = (d["dl"].astype(np.float32) * np.float32(256)).astype(BF); return d
def setup_inputs_spread(rng):
    d = setup_inputs(rng); d["wm"] = wide(rng, N, 128, 4 * SH, cols=8); d["dl"] = wide(rng, N, 128, (RD - 1) * 4 * CH, cols=8); return d
def check_inputs(d):
    b = []
    for r in range(N):
        e = entries(d["idx"][r])
        if e.min() < 0 or e.max() >= SH: b.append("idx: range")
        for t in range(1, RD):
            if len(set(e[CH * (t - 1):CH * t].tolist())) != CH: b.append("idx: a column twice in one round")
    return b
def reference(wm, dl, idx, x):
    W = []
    for q in range(N):
        m = wm[q].reshape(128, SH, 4).copy(); d = dl[q].reshape(128, (RD - 1) * CH, 4); e = entries(idx[q])
        W.append([mx_ref.quantize(wm[q])])
        for t in range(1, RD):
            s = slice(CH * (t - 1), CH * t)
            m[:, e[s]] = (m[:, e[s]].astype(np.float32) + np.float32(0.25) * d[:, s].astype(np.float32)).astype(BF)
            W[q].append(mx_ref.quantize(m.reshape(128, 4 * SH).copy()))
    y = np.zeros((N, 128, RD * N * SH), np.float32)
    for r in range(N):
        for t in range(RD):
            X = mx_ref.quantize(np.ascontiguousarray(x[r][:, 512 * t:512 * t + 512]))
            for q in range(N):
                k = t * N + q
                y[r][:, SH * k:SH * k + SH] = mx_ref.matmul(X, W[q][t])
    return {"y": y}

@@ -1,0 +1,332 @@
+from concourse.bass import DstId, RemoteDMATransfer
+from concourse.mybir import dt, AluOpType, AxisListType, ActivationFunctionType
+
+SCRATCH = {
+    "m": ("sbuf", [128, 1280], "bfloat16"),
+    "dlb": ("sbuf", [128, 768], "bfloat16"),
+    "dq": ("sbuf", [128, 768], "bfloat16"),
+    "ltab": ("sbuf", [128, 12], "int32"),
+    "lrow": ("sbuf", [1, 192], "int32"),
+    "lb": ("sbuf", [128, 192], "int32"),
+    "pc": ("sbuf", [128, 192], "float32"),
+    "pcs": ("sbuf", [128, 192], "float32"),
+    "kk": ("sbuf", [128, 192], "float32"),
+    "v2": ("sbuf", [128, 260], "bfloat16"),
+    "v3": ("sbuf", [128, 516], "bfloat16"),
+    "r2": ("sbuf", [128, 260], "bfloat16"),
+    "r3": ("sbuf", [128, 516], "bfloat16"),
+    "s2": ("sbuf", [128, 260], "bfloat16"),
+    "s3": ("sbuf", [128, 516], "bfloat16"),
+    "vs": ("sbuf", [128, 192], "float32"),
+    "vm": ("sbuf", [128, 192], "float32"),
+    "bi": ("sbuf", [128, 8], "float32"),
+    "o1": ("sbuf", [128, 4], "uint16"),
+    "o2": ("sbuf", [128, 4], "uint16"),
+    "o3": ("sbuf", [128, 4], "uint16"),
+    "pi": ("sbuf", [128, 1], "int32"),
+    "pa": ("sbuf", [128, 1], "int32"),
+    "pb": ("sbuf", [128, 1], "int32"),
+    "pf": ("sbuf", [128, 1], "float32"),
+    "pj": ("sbuf", [128, 1], "float32"),
+    "bis": ("sbuf", [128, 1], "float32"),
+    "bas": ("sbuf", [128, 1], "float32"),
+    "sown": ("sbuf", [128, 3], "uint16"),
+    "lst": ("sbuf", [128, 12], "uint16"),
+    "tab": ("sbuf", [128, 96], "uint16"),
+    "tabt": ("sbuf", [128, 96], "uint16"),
+    "cb": ("sbuf", [128, 512], "float8_e4m3fn_x4"),
+    "sb": ("sbuf", [128, 512], "uint8"),
+    "cd": ("sbuf", [128, 768], "float8_e4m3fn_x4"),
+    "sd": ("sbuf", [128, 768], "uint8"),
+    "xb": ("sbuf", [128, 2048], "bfloat16"),
+    "xq": ("sbuf", [128, 512], "float8_e4m3fn_x4"),
+    "xs": ("sbuf", [128, 512], "uint8"),
+    "yb": ("sbuf", [128, 2048], "float32"),
+    "ps": ("psum", [128, 4096], "float32"),
+}
+for _t in (1, 2, 3):
+    for _p in (0, 1):
+        SCRATCH["w%d%d" % (_t, _p)] = ("sbuf", [128, 640], "float32")
+
+SEMAPHORES = (["%s%d" % (n, q) for n in ("base", "chg", "lst") for q in range(4)]
+              + ["sent", "ldw", "ldt", "ldr1", "ldr", "ldd", "ldx", "iot", "bc1", "bc2", "fill", "rz", "rs", "pcs", "pab", "pf",
+                 "pj", "bis", "tb1", "tb2", "ba", "dq1", "dq2", "dq3", "qb", "qd", "kk1", "kk2", "va", "vb", "s2", "o2",
+                 "s3", "o3", "g1", "g2", "g3", "vs", "vm", "own", "ownd", "rep", "st"]
+              + ["%s%d" % (n, t) for n in ("qx", "pb", "cb") for t in range(4)]
+              + ["%s%d%d" % (n, t, p) for n in ("pd", "cd", "ga", "tt") for t in (1, 2, 3) for p in (0, 1)])
+
+OP = AluOpType
+AF = ActivationFunctionType
+SH, CH, RD = 128, 64, 4
+LARGE = 2.0 ** 20
+
+
+def rank_program(g, core, T, topo):
+    rank = T.rank_of(core)
+    if rank is None:
+        return
+    S = T.sem
+    V, A, PE, SY = g.vector, g.scalar, g.tensor, g.sync
+    peers = [c for c in T.cores if c != core]
+    near = [c for c in peers if c in topo.cores_of(core)]
+    far = [c for c in peers if c not in topo.cores_of(core)]
+    near_r = [T.rank_of(c) for c in near]
+    far_r = [T.rank_of(c) for c in far]
+    far_e = topo.engines(core, far[0])
+    near_e = [e for e in topo.engines(core, near[0]) if e not in far_e][:len(far_e) * len(near) // len(far)]
+    half = rank % 2
+    mine, other = rank // 2, 1 - rank // 2
+
+    def ids(cores):
+        out = []
+        for c in cores:
+            rid, pid = topo.addr(c, core)
+            out.append(DstId(rid=rid, pnc=pid))
+        return out
+
+    def bits(engs):
+        return sum(1 << e for e in engs)
+
+    def send(dst, src, sem):
+        g.remote_dma_fused([
+            RemoteDMATransfer(dst_ids=ids(far), dma_engine_mask=bits(far_e), remote_sem=S[sem], srcs=[src], dsts=[dst] * len(far)),
+            RemoteDMATransfer(dst_ids=ids(near), dma_engine_mask=bits(near_e), remote_sem=S[sem], srcs=[src], dsts=[dst] * len(near)),
+        ], local_sem=S["sent"])
+        return len(far_e) + len(near_e)
+
+    nb = {}
+    for q in far_r:
+        nb[q] = len(far_e)
+    for q in near_r:
+        nb[q] = len(near_e)
+    cbv, sbv = T.cb[:, SH * rank:SH * rank + SH], T.sb[:, SH * rank:SH * rank + SH]
+    cdv, sdv = T.cd[:, 192 * rank:192 * rank + 192], T.sd[:, 192 * rank:192 * rank + 192]
+
+    def row(t):
+        A.dma_start(T.lrow[0:1, CH * (t - 1):CH * t], T.idx[:, 4 * (t - 1):4 * t]).then_inc(S["ldr1" if t == 1 else "ldr"], 16)
+
+    SY.dma_start(T.m[:, 768:1280], T.wm[:]).then_inc(S["ldw"], 16)
+    row(1)
+    A.dma_start(T.dlb[:], T.dl[:]).then_inc(S["ldd"], 16)
+    row(2)
+    row(3)
+    for k in range(5):
+        SY.dma_start(T.ltab[16 * k:16 * k + 16, :], T.idx[:]).then_inc(S["ldt"], 16)
+    for k in range(5, 8):
+        A.dma_start(T.ltab[16 * k:16 * k + 16, :], T.idx[:]).then_inc(S["ldt"], 16)
+    SY.dma_start(T.xb[:], T.x[:]).then_inc(S["ldx"], 16)
+
+    g.iota(T.pi[:], [[0, 1]], 0, 1).then_inc(S["iot"], 1)
+    g.iota(T.pc[:], [[-CH, 3], [1, 16], [16, 4]], 128, 0, allow_small_or_imprecise_dtypes=True).then_inc(S["iot"], 1)
+    g.wait_ge(S["ldr1"], 16)
+    g.partition_broadcast(T.lb[:, 0:CH], T.lrow[0:1, 0:CH], 128).then_inc(S["bc1"], 1)
+    g.wait_ge(S["ldr"], 32)
+    g.partition_broadcast(T.lb[:, CH:192], T.lrow[0:1, CH:192], 128).then_inc(S["bc2"], 1)
+    sent = 0
+    g.wait_ge(S["qb"], 1)
+    sent += send(cbv.bitcast(dt.uint8), cbv.bitcast(dt.uint8), "base%d" % rank)
+    g.wait_ge(S["own"], 1)
+    sent += send(T.lst[:, 3 * rank:3 * rank + 3], T.sown[:], "lst%d" % rank)
+    sent += send(sbv, sbv, "base%d" % rank)
+    g.wait_ge(S["qd"], 1)
+    sent += send(cdv.bitcast(dt.uint8), cdv.bitcast(dt.uint8), "chg%d" % rank)
+    sent += send(sdv, sdv, "chg%d" % rank)
+    g.wait_ge(S["sent"], sent)
+
+    V.memset(T.r2[:], 0.0).then_inc(S["rz"], 1)
+    V.memset(T.r3[:], 0.0).then_inc(S["rz"], 1)
+    V.memset(T.w10[:, 192:320], 0.0).then_inc(S["fill"], 1)
+    V.memset(T.w11[:, 192:320], 0.0).then_inc(S["fill"], 1)
+    V.wait_ge(S["iot"], 2)
+    V.tensor_scalar(T.pcs[:], T.pc[:], 1.0 / 4096, None, OP.mult).then_inc(S["pcs"], 1)
+    V.tensor_scalar(T.pa[:], T.pi[:], 7, None, OP.bitwise_and).then_inc(S["pab"], 1)
+    V.tensor_scalar(T.pb[:], T.pi[:], 3, None, OP.logical_shift_right).then_inc(S["pab"], 1)
+    V.wait_ge(S["rz"], 2)
+    V.memset(T.r2[:, 0:260:65], LARGE).then_inc(S["rs"], 1)
+    V.memset(T.r3[:, 0:516:129], LARGE).then_inc(S["rs"], 1)
+    V.wait_ge(S["pab"], 2)
+    V.tensor_scalar(T.pf[:], T.pa[:], 16.0, None, OP.mult).then_inc(S["pf"], 1)
+    V.wait_ge(S["pf"], 1)
+    V.tensor_tensor(T.pj[:], T.pf[:], T.pb[:], OP.add).then_inc(S["pj"], 1)
+    V.wait_ge(S["pj"], 1)
+    V.tensor_scalar(T.bis[:], T.pj[:], -4096.0, float(192 * half), OP.mult, OP.add).then_inc(S["bis"], 1)
+    V.tensor_scalar(T.bas[:], T.pj[:], float(384 + SH * half), None, OP.add).then_inc(S["bis"], 1)
+    V.wait_ge(S["bis"], 2)
+    V.wait_ge(S["rs"], 2)
+    V.wait_ge(S["fill"], 2)
+    V.wait_ge(S["pcs"], 1)
+    V.wait_ge(S["ldw"], 16)
+    V.quantize_mx(cbv, sbv, T.m[:, 768:1280]).then_inc(S["qb"], 1)
+    V.wait_ge(S["ldt"], 128)
+    V.tensor_scalar(T.bi[:], T.ltab[:, 4:12], -4096.0, -64.0, OP.mult, OP.add).then_inc(S["tb2"], 1)
+    V.tensor_scalar(T.o1[:], T.ltab[:, 0:4], 4.0, None, OP.mult).then_inc(S["tb1"], 1)
+    V.tensor_scalar(T.v2[:, 64:260:65], T.ltab[:, 4:8], 128.0, None, OP.add).then_inc(S["ba"], 1)
+    V.tensor_scalar(T.v3[:, 128:516:129], T.ltab[:, 8:12], 128.0, None, OP.add).then_inc(S["ba"], 1)
+    V.wait_ge(S["bc1"], 1)
+    V.tensor_tensor(T.kk[:, 0:CH], T.lb[:, 0:CH], T.pcs[:, 0:CH], OP.add).then_inc(S["kk1"], 1)
+
+    def make(t, off, *es):
+        lo = 256 * (RD - t)
+        for e in es:
+            V.tensor_tensor(T.m[:, lo - 256 + e:lo:4], T.m[:, lo + e:1280].indirect(off[:, 0:4]),
+                            T.dq[:, 256 * (t - 1) + e:256 * t:4], OP.add).then_inc(S["g%d" % t], 1)
+
+    V.wait_ge(S["tb1"], 1)
+    V.wait_ge(S["dq1"], 1)
+    make(1, T.o1, 0, 1, 2)
+    V.wait_ge(S["bc2"], 1)
+    V.tensor_tensor(T.kk[:, CH:192], T.lb[:, CH:192], T.pcs[:, CH:192], OP.add).then_inc(S["kk2"], 1)
+    V.wait_ge(S["ba"], 2)
+    V.wait_ge(S["va"], 4)
+    V.tensor_tensor_scan(T.s2[:], T.r2[:], T.v2[:], 2 * LARGE, OP.add, OP.min).then_inc(S["s2"], 1)
+    make(1, T.o1, 3)
+    V.wait_ge(S["s2"], 1)
+    V.tensor_scalar(T.o2[:], T.s2[:, 64:260:65], 4.0, -256.0, OP.mult, OP.add).then_inc(S["o2"], 1)
+    V.wait_ge(S["vs"], 1)
+    V.tensor_tensor_scan(T.vm[:], T.vs[:], T.vs[:], 1.0e9, OP.min, OP.min).then_inc(S["vm"], 1)
+    V.wait_ge(S["o2"], 1)
+    V.wait_ge(S["g1"], 4)
+    V.wait_ge(S["dq2"], 1)
+    V.wait_ge(S["vm"], 1)
+    V.tensor_scalar(T.sown[:], T.vm[:, CH - 1:192:CH], T.bas[:], None, OP.min).then_inc(S["own"], 1)
+    make(2, T.o2, 0, 1)
+    V.wait_ge(S["vb"], 4)
+    V.tensor_tensor_scan(T.s3[:], T.r3[:], T.v3[:], 2 * LARGE, OP.add, OP.min).then_inc(S["s3"], 1)
+    make(2, T.o2, 2)
+    V.wait_ge(S["s3"], 1)
+    V.tensor_scalar(T.o3[:], T.s3[:, 128:516:129], 4.0, None, OP.mult).then_inc(S["o3"], 1)
+    make(2, T.o2, 3)
+    V.wait_ge(S["o3"], 1)
+    V.wait_ge(S["dq3"], 1)
+    V.wait_ge(S["g2"], 4)
+    make(3, T.o3, 0, 1, 2, 3)
+    V.wait_ge(S["g3"], 4)
+    V.quantize_mx(cdv, sdv, T.m[:, 0:768]).then_inc(S["qd"], 1)
+    V.wait_ge(S["ldx"], 16)
+    for t in range(RD):
+        V.quantize_mx(T.xq[:, SH * t:SH * t + SH], T.xs[:, SH * t:SH * t + SH], T.xb[:, 512 * t:512 * t + 512]).then_inc(S["qx%d" % t], 1)
+
+    def quarter(t):
+        A.activation(T.dq[:, 256 * (t - 1):256 * t], T.dlb[:, 256 * (t - 1):256 * t], AF.Copy, scale=0.25).then_inc(S["dq%d" % t], 1)
+
+    A.wait_ge(S["ldd"], 16)
+    quarter(1)
+    A.wait_ge(S["tb2"], 1)
+    A.wait_ge(S["kk1"], 1)
+    for s in range(4):
+        A.activation(T.v2[:, 65 * s:65 * s + CH], T.kk[:, 0:CH], AF.Abs, bias=T.bi[:, s:s + 1], scale=4096.0).then_inc(S["va"], 1)
+    quarter(2)
+    A.wait_ge(S["kk2"], 1)
+    A.wait_ge(S["bis"], 2)
+    A.activation(T.vs[:], T.kk[:], AF.Abs, bias=T.bis[:], scale=4096.0).then_inc(S["vs"], 1)
+    for s in range(4):
+        A.activation(T.v3[:, 129 * s:129 * s + 128], T.kk[:, 0:128], AF.Abs, bias=T.bi[:, 4 + s:5 + s], scale=4096.0).then_inc(S["vb"], 1)
+    quarter(3)
+
+    def bank(k, n):
+        return T.ps[:, 512 * k:512 * k + n]
+
+    def xt(t):
+        return T.xq[:, SH * t:SH * t + SH], T.xs[:, SH * t:SH * t + SH]
+
+    PE.wait_ge(S["qb"], 1)
+    for q in near_r + far_r:
+        PE.wait_ge(S["base%d" % q], 2 * nb[q])
+    for t in range(RD):
+        PE.wait_ge(S["qx%d" % t], 1)
+        PE.matmul_mx(bank(t, 512), xt(t)[0], xt(t)[1], T.cb[:], T.sb[:], True, True).then_inc(S["pb%d" % t], 1)
+    banks = {(1, mine): 4, (2, mine): 5, (3, mine): 6, (1, other): 7, (2, other): 0, (3, other): 1}
+    first = {1: 128, 2: 64, 3: 0}
+
+    def changed(p):
+        for t in (1, 2, 3):
+            k = banks[(t, p)]
+            if k < RD:
+                PE.wait_ge(S["cb%d" % k], 1 if k == 0 else 2)
+            lo, hi = 384 * p + first[t], 384 * p + 384
+            PE.matmul_mx(bank(k, hi - lo), xt(t)[0], xt(t)[1], T.cd[:, lo:hi], T.sd[:, lo:hi], True, True).then_inc(S["pd%d%d" % (t, p)], 1)
+
+    PE.wait_ge(S["qd"], 1)
+    for q in near_r:
+        PE.wait_ge(S["chg%d" % q], 2 * nb[q])
+    changed(mine)
+    for q in far_r:
+        PE.wait_ge(S["chg%d" % q], 2 * nb[q])
+    changed(other)
+
+    def vcopy(out, in_):
+        return V.tensor_copy(out, in_)
+
+    def acopy(out, in_):
+        return A.activation(out, in_, AF.Copy)
+
+    def base_copy(q, cp, t):
+        q.wait_ge(S["pb%d" % t], 1)
+        if t == 0:
+            cp(T.yb[:, 0:512], bank(0, 512)).then_inc(S["cb0"], 1)
+            return
+        for p in (0, 1):
+            cp(T["w%d%d" % (t, p)][:, 384:640], T.ps[:, 512 * t + 256 * p:512 * t + 256 * p + 256]).then_inc(S["cb%d" % t], 1)
+
+    def changed_copy(q, cp, t, p):
+        q.wait_ge(S["pd%d%d" % (t, p)], 1)
+        k, w, f = 512 * banks[(t, p)], T["w%d%d" % (t, p)], first[t]
+        if t > 1:
+            cp(w[:, f:384], T.ps[:, k:k + 384 - f]).then_inc(S["cd%d%d" % (t, p)], 1)
+            return
+        for h in (f, f + 192):
+            cp(w[:, h:h + CH], T.ps[:, k + h - f:k + h - f + CH]).then_inc(S["cd%d%d" % (t, p)], 1)
+
+    def order(t, p):
+        for h in (0, 1):
+            q = 2 * p + h
+            k = 8 * (4 * (t - 1) + q)
+            V.tensor_scalar(T.tabt[:, k:k + 8], T.tab[:, 3 * q + t - 1:96:12], -float(first[t]), None, OP.add).then_inc(S["tt%d%d" % (t, p)], 1)
+
+    def pick(q, cp, t, p, lo=0, hi=2):
+        q.wait_ge(S["tt%d%d" % (t, p)], 2)
+        q.wait_ge(S["cb%d" % t], 2)
+        q.wait_ge(S["cd%d%d" % (t, p)], 2 if t == 1 else 1)
+        k, c = 8 * (4 * (t - 1) + 2 * p), 512 * t + 256 * p
+        cp(T.yb[:, c + SH * lo:c + SH * hi],
+           T["w%d%d" % (t, p)][:, first[t]:640].indirect(T.tabt[:, k + 8 * lo:k + 8 * hi])).then_inc(S["ga%d%d" % (t, p)], hi - lo)
+
+    base_copy(A, acopy, 0)
+    A.wait_ge(S["cb0"], 1)
+    A.dma_start(T.y[:, 0:512], T.yb[:, 0:512]).then_inc(S["st"], 16)
+    base_copy(A, acopy, 2)
+    changed_copy(A, acopy, 1, mine)
+    changed_copy(A, acopy, 2, mine)
+    pick(A, acopy, 1, mine)
+    pick(A, acopy, 2, mine)
+    changed_copy(A, acopy, 1, other)
+    pick(A, acopy, 1, other)
+    pick(A, acopy, 2, other, 1, 2)
+    pick(A, acopy, 3, other, 1, 2)
+    base_copy(V, vcopy, 1)
+    base_copy(V, vcopy, 3)
+    changed_copy(V, vcopy, 3, mine)
+    V.wait_ge(S["rep"], 128)
+    for t in (1, 2, 3):
+        order(t, mine)
+    pick(V, vcopy, 3, mine)
+    for t in (1, 2, 3):
+        order(t, other)
+    changed_copy(V, vcopy, 2, other)
+    changed_copy(V, vcopy, 3, other)
+    pick(V, vcopy, 2, other, 0, 1)
+    pick(V, vcopy, 3, other, 0, 1)
+
+    SY.wait_ge(S["own"], 1)
+    SY.dma_start(T.lst[:, 3 * rank:3 * rank + 3], T.sown[:]).then_inc(S["ownd"], 16)
+    SY.wait_ge(S["ownd"], 16)
+    for q in near_r + far_r:
+        SY.wait_ge(S["lst%d" % q], nb[q])
+    for k in range(8):
+        SY.dma_start(T.tab[16 * k:16 * k + 16, :], T.lst[:]).then_inc(S["rep"], 16)
+    for p, turn in ((mine, (1, 3, 2)), (other, (1, 2, 3))):
+        for t in turn:
+            SY.wait_ge(S["ga%d%d" % (t, p)], 2)
+            c = 512 * t + 256 * p
+            SY.dma_start(T.y[:, c:c + 256], T.yb[:, c:c + 256]).then_inc(S["st"], 16)
+    SY.wait_ge(S["st"], 16 * 7)

@@ -6,33 +6,35 @@ SCRATCH = {
     "dlb": ("sbuf", [128, 768], "bfloat16"),
     "dq": ("sbuf", [128, 768], "bfloat16"),
     "ltab": ("sbuf", [128, 12], "int32"),
-    "lrow": ("sbuf", [1, 192], "int32"),
-    "lb": ("sbuf", [128, 192], "int32"),
-    "pc": ("sbuf", [128, 192], "float32"),
-    "pcs": ("sbuf", [128, 192], "float32"),
-    "kk": ("sbuf", [128, 192], "float32"),
+    "u4": ("sbuf", [128, 12], "uint16"),
+    "num": ("sbuf", [128, 512], "bfloat16"),
+    "lr": ("sbuf", [128, 128], "float32"),
+    "bi": ("sbuf", [128, 8], "float32"),
     "v2": ("sbuf", [128, 260], "bfloat16"),
     "v3": ("sbuf", [128, 516], "bfloat16"),
     "r2": ("sbuf", [128, 260], "bfloat16"),
     "r3": ("sbuf", [128, 516], "bfloat16"),
     "s2": ("sbuf", [128, 260], "bfloat16"),
     "s3": ("sbuf", [128, 516], "bfloat16"),
-    "vs": ("sbuf", [128, 192], "float32"),
-    "vm": ("sbuf", [128, 192], "float32"),
-    "bi": ("sbuf", [128, 8], "float32"),
-    "o1": ("sbuf", [128, 4], "uint16"),
+    "vs": ("sbuf", [128, 198], "bfloat16"),
+    "rs": ("sbuf", [128, 198], "bfloat16"),
+    "vm": ("sbuf", [128, 198], "bfloat16"),
+    "zero": ("sbuf", [128, 4], "bfloat16"),
     "o2": ("sbuf", [128, 4], "uint16"),
     "o3": ("sbuf", [128, 4], "uint16"),
     "pi": ("sbuf", [128, 1], "int32"),
-    "pa": ("sbuf", [128, 1], "int32"),
     "pb": ("sbuf", [128, 1], "int32"),
-    "pf": ("sbuf", [128, 1], "float32"),
+    "pc": ("sbuf", [128, 1], "int32"),
+    "pg": ("sbuf", [128, 1], "float32"),
+    "ph": ("sbuf", [128, 1], "float32"),
     "pj": ("sbuf", [128, 1], "float32"),
     "bis": ("sbuf", [128, 1], "float32"),
-    "bas": ("sbuf", [128, 1], "float32"),
-    "sown": ("sbuf", [128, 3], "uint16"),
-    "lst": ("sbuf", [128, 12], "uint16"),
-    "tab": ("sbuf", [128, 96], "uint16"),
+    "ini": ("sbuf", [128, 1], "float32"),
+    "sown": ("sbuf", [128, 3], "bfloat16"),
+    "lst": ("sbuf", [128, 12], "bfloat16"),
+    "tab": ("sbuf", [128, 96], "bfloat16"),
+    "six": ("sbuf", [128, 6], "float32"),
+    "turn": ("sbuf", [128, 6], "uint16"),
     "tabt": ("sbuf", [128, 96], "uint16"),
     "cb": ("sbuf", [128, 512], "float8_e4m3fn_x4"),
     "sb": ("sbuf", [128, 512], "uint8"),
@@ -45,20 +47,23 @@ SCRATCH = {
     "ps": ("psum", [128, 4096], "float32"),
 }
 for _t in (1, 2, 3):
-    for _p in (0, 1):
-        SCRATCH["w%d%d" % (_t, _p)] = ("sbuf", [128, 640], "float32")
+    for _q in range(4):
+        SCRATCH["w%d%d" % (_t, _q)] = ("sbuf", [128, 128 + 64 * _t], "float32")
 
-SEMAPHORES = (["%s%d" % (n, q) for n in ("base", "chg", "lst") for q in range(4)]
-              + ["sent", "ldw", "ldt", "ldr1", "ldr", "ldd", "ldx", "iot", "bc1", "bc2", "fill", "rz", "rs", "pcs", "pab", "pf",
-                 "pj", "bis", "tb1", "tb2", "ba", "dq1", "dq2", "dq3", "qb", "qd", "kk1", "kk2", "va", "vb", "s2", "o2",
-                 "s3", "o3", "g1", "g2", "g3", "vs", "vm", "own", "ownd", "rep", "st"]
-              + ["%s%d" % (n, t) for n in ("qx", "pb", "cb") for t in range(4)]
-              + ["%s%d%d" % (n, t, p) for n in ("pd", "cd", "ga", "tt") for t in (1, 2, 3) for p in (0, 1)])
+PRODUCTS = 24
+SEMAPHORES = (["%s%s" % (piece, who) for piece in ("c1", "p1", "c2", "p2") for who in ("mate", "twin", "diag")]
+              + ["lst", "sent", "ldw", "ldt", "ld1", "ld2", "ldx", "iot", "nz", "num", "rz", "rs", "pab", "pf", "ini", "bis", "turn",
+                 "u4", "bi", "ba", "dq1", "dq2", "dq3", "q1", "q2", "lr", "va", "vb", "s2", "o2",
+                 "s3", "o3", "g1", "g2", "g3", "vs", "vm", "own", "ownd", "rep", "dup", "tt", "st"]
+              + ["qx%d" % t for t in range(4)]
+              + ["%s%d" % (n, j) for n in ("made", "out") for j in range(PRODUCTS)]
+              + ["ga%d%d" % (t, q) for t in (1, 2, 3) for q in range(4)])
 
 OP = AluOpType
 AF = ActivationFunctionType
 SH, CH, RD = 128, 64, 4
 LARGE = 2.0 ** 20
+FAR = 2048.0
 
 
 def rank_program(g, core, T, topo):
@@ -68,265 +73,274 @@ def rank_program(g, core, T, topo):
     S = T.sem
     V, A, PE, SY = g.vector, g.scalar, g.tensor, g.sync
     peers = [c for c in T.cores if c != core]
-    near = [c for c in peers if c in topo.cores_of(core)]
-    far = [c for c in peers if c not in topo.cores_of(core)]
-    near_r = [T.rank_of(c) for c in near]
-    far_r = [T.rank_of(c) for c in far]
-    far_e = topo.engines(core, far[0])
-    near_e = [e for e in topo.engines(core, near[0]) if e not in far_e][:len(far_e) * len(near) // len(far)]
-    half = rank % 2
-    mine, other = rank // 2, 1 - rank // 2
+    mate_c = [c for c in peers if c in topo.cores_of(core)][0]
+    twin_c = [c for c in peers if c != mate_c and topo.die(c) == topo.die(core)][0]
+    diag_c = [c for c in peers if c not in (mate_c, twin_c)][0]
+    mate, twin, diag = T.rank_of(mate_c), T.rank_of(twin_c), T.rank_of(diag_c)
+    far_e = topo.engines(core, twin_c)
+    chip_e = [e for e in topo.engines(core, mate_c) if e not in far_e]
+    near_e = chip_e[0::2]
+    on_e = {"1": chip_e[1::2], "2": far_e}
 
-    def ids(cores):
-        out = []
+    def transfer(cores, engs, sem, dst, src):
+        ids = []
         for c in cores:
             rid, pid = topo.addr(c, core)
-            out.append(DstId(rid=rid, pnc=pid))
-        return out
+            ids.append(DstId(rid=rid, pnc=pid))
+        return RemoteDMATransfer(dst_ids=ids, dma_engine_mask=sum(1 << e for e in engs), remote_sem=S[sem], srcs=[src], dsts=[dst] * len(cores))
 
-    def bits(engs):
-        return sum(1 << e for e in engs)
+    def view(piece, q):
+        if piece == "c1":
+            return T.cb[:, SH * q:SH * q + SH].bitcast(dt.uint8)
+        if piece == "p1":
+            return T.sb[:, SH * q:SH * q + SH]
+        if piece == "c2":
+            return T.cd[:, 192 * q:192 * q + 192].bitcast(dt.uint8)
+        return T.sd[:, 192 * q:192 * q + 192]
 
-    def send(dst, src, sem):
-        g.remote_dma_fused([
-            RemoteDMATransfer(dst_ids=ids(far), dma_engine_mask=bits(far_e), remote_sem=S[sem], srcs=[src], dsts=[dst] * len(far)),
-            RemoteDMATransfer(dst_ids=ids(near), dma_engine_mask=bits(near_e), remote_sem=S[sem], srcs=[src], dsts=[dst] * len(near)),
-        ], local_sem=S["sent"])
+    def send(piece):
+        v = view(piece, rank)
+        g.remote_dma_fused([transfer([twin_c], far_e, piece + "twin", v, v), transfer([mate_c], near_e, piece + "mate", v, v)], local_sem=S["sent"])
         return len(far_e) + len(near_e)
 
-    nb = {}
-    for q in far_r:
-        nb[q] = len(far_e)
-    for q in near_r:
-        nb[q] = len(near_e)
-    cbv, sbv = T.cb[:, SH * rank:SH * rank + SH], T.sb[:, SH * rank:SH * rank + SH]
-    cdv, sdv = T.cd[:, 192 * rank:192 * rank + 192], T.sd[:, 192 * rank:192 * rank + 192]
+    def landed(q, piece, who):
+        q.wait_ge(S[piece + who], len({"mate": near_e, "twin": far_e, "diag": on_e[piece[1]]}[who]))
 
-    def row(t):
-        A.dma_start(T.lrow[0:1, CH * (t - 1):CH * t], T.idx[:, 4 * (t - 1):4 * t]).then_inc(S["ldr1" if t == 1 else "ldr"], 16)
+    def hand_on(piece):
+        landed(g, piece, "twin")
+        v = view(piece, twin)
+        g.remote_dma_fused([transfer([mate_c], on_e[piece[1]], piece + "diag", v, v)], local_sem=S["sent"])
+        return len(on_e[piece[1]])
 
-    SY.dma_start(T.m[:, 768:1280], T.wm[:]).then_inc(S["ldw"], 16)
-    row(1)
-    A.dma_start(T.dlb[:], T.dl[:]).then_inc(S["ldd"], 16)
-    row(2)
-    row(3)
-    for k in range(5):
-        SY.dma_start(T.ltab[16 * k:16 * k + 16, :], T.idx[:]).then_inc(S["ldt"], 16)
-    for k in range(5, 8):
-        A.dma_start(T.ltab[16 * k:16 * k + 16, :], T.idx[:]).then_inc(S["ldt"], 16)
+    SY.dma_start(T.m[:, 0:512], T.wm[:]).then_inc(S["ldw"], 16)
+    for k in range(8):
+        (SY if k < 4 else A).dma_start(T.ltab[16 * k:16 * k + 16, :], T.idx[:]).then_inc(S["ldt"], 16)
+    A.dma_start(T.dlb[:, 0:256], T.dl[:, 0:256]).then_inc(S["ld1"], 16)
+    A.dma_start(T.dlb[:, 256:768], T.dl[:, 256:768]).then_inc(S["ld2"], 16)
     SY.dma_start(T.xb[:], T.x[:]).then_inc(S["ldx"], 16)
 
     g.iota(T.pi[:], [[0, 1]], 0, 1).then_inc(S["iot"], 1)
-    g.iota(T.pc[:], [[-CH, 3], [1, 16], [16, 4]], 128, 0, allow_small_or_imprecise_dtypes=True).then_inc(S["iot"], 1)
-    g.wait_ge(S["ldr1"], 16)
-    g.partition_broadcast(T.lb[:, 0:CH], T.lrow[0:1, 0:CH], 128).then_inc(S["bc1"], 1)
-    g.wait_ge(S["ldr"], 32)
-    g.partition_broadcast(T.lb[:, CH:192], T.lrow[0:1, CH:192], 128).then_inc(S["bc2"], 1)
+    g.iota(T.pj[:], [[0, 1]], SH - 1, -16, allow_small_or_imprecise_dtypes=True).then_inc(S["iot"], 1)
+    g.iota(T.six[:], [[1, 3], [6, 2]], 0, 12, allow_small_or_imprecise_dtypes=True).then_inc(S["iot"], 1)
+    g.wait_ge(S["nz"], 1)
+    g.iota(T.num[:, 0:512:4], [[1, SH]], 0, 0, allow_small_or_imprecise_dtypes=True).then_inc(S["num"], 1)
     sent = 0
-    g.wait_ge(S["qb"], 1)
-    sent += send(cbv.bitcast(dt.uint8), cbv.bitcast(dt.uint8), "base%d" % rank)
+    g.wait_ge(S["q1"], 1)
+    sent += send("c1")
     g.wait_ge(S["own"], 1)
-    sent += send(T.lst[:, 3 * rank:3 * rank + 3], T.sown[:], "lst%d" % rank)
-    sent += send(sbv, sbv, "base%d" % rank)
-    g.wait_ge(S["qd"], 1)
-    sent += send(cdv.bitcast(dt.uint8), cdv.bitcast(dt.uint8), "chg%d" % rank)
-    sent += send(sdv, sdv, "chg%d" % rank)
+    slot = T.lst[:, 3 * rank:3 * rank + 3]
+    g.remote_dma_fused([transfer([twin_c, diag_c], far_e, "lst", slot, T.sown[:]), transfer([mate_c], near_e, "lst", slot, T.sown[:])], local_sem=S["sent"])
+    sent += len(far_e) + len(near_e)
+    sent += send("p1")
+    g.wait_ge(S["q2"], 1)
+    sent += send("c2")
+    sent += send("p2")
+    for piece in ("c1", "p1", "c2", "p2"):
+        sent += hand_on(piece)
     g.wait_ge(S["sent"], sent)
 
-    V.memset(T.r2[:], 0.0).then_inc(S["rz"], 1)
-    V.memset(T.r3[:], 0.0).then_inc(S["rz"], 1)
-    V.memset(T.w10[:, 192:320], 0.0).then_inc(S["fill"], 1)
-    V.memset(T.w11[:, 192:320], 0.0).then_inc(S["fill"], 1)
-    V.wait_ge(S["iot"], 2)
-    V.tensor_scalar(T.pcs[:], T.pc[:], 1.0 / 4096, None, OP.mult).then_inc(S["pcs"], 1)
-    V.tensor_scalar(T.pa[:], T.pi[:], 7, None, OP.bitwise_and).then_inc(S["pab"], 1)
+    V.memset(T.num[:], 0.0).then_inc(S["nz"], 1)
+    V.memset(T.r2[:], 4.0).then_inc(S["rz"], 1)
+    V.memset(T.r3[:], 4.0).then_inc(S["rz"], 1)
+    V.memset(T.zero[:], 0.0).then_inc(S["rz"], 1)
+    V.wait_ge(S["iot"], 3)
     V.tensor_scalar(T.pb[:], T.pi[:], 3, None, OP.logical_shift_right).then_inc(S["pab"], 1)
-    V.wait_ge(S["rz"], 2)
-    V.memset(T.r2[:, 0:260:65], LARGE).then_inc(S["rs"], 1)
-    V.memset(T.r3[:, 0:516:129], LARGE).then_inc(S["rs"], 1)
-    V.wait_ge(S["pab"], 2)
-    V.tensor_scalar(T.pf[:], T.pa[:], 16.0, None, OP.mult).then_inc(S["pf"], 1)
-    V.wait_ge(S["pf"], 1)
-    V.tensor_tensor(T.pj[:], T.pf[:], T.pb[:], OP.add).then_inc(S["pj"], 1)
-    V.wait_ge(S["pj"], 1)
-    V.tensor_scalar(T.bis[:], T.pj[:], -4096.0, float(192 * half), OP.mult, OP.add).then_inc(S["bis"], 1)
-    V.tensor_scalar(T.bas[:], T.pj[:], float(384 + SH * half), None, OP.add).then_inc(S["bis"], 1)
-    V.wait_ge(S["bis"], 2)
-    V.wait_ge(S["rs"], 2)
-    V.wait_ge(S["fill"], 2)
-    V.wait_ge(S["pcs"], 1)
+    V.memset(T.rs[:], 1.0).then_inc(S["rz"], 1)
+    V.wait_ge(S["pab"], 1)
+    V.tensor_scalar(T.ini[:], T.pb[:], 127.0, T.pj[:], OP.mult, OP.add).then_inc(S["ini"], 1)
+    V.wait_ge(S["ini"], 1)
+    V.tensor_scalar(T.bis[:], T.ini[:], -127.0, FAR, OP.add, OP.mult).then_inc(S["bis"], 1)
     V.wait_ge(S["ldw"], 16)
-    V.quantize_mx(cbv, sbv, T.m[:, 768:1280]).then_inc(S["qb"], 1)
+    V.quantize_mx(T.cb[:, SH * rank:SH * rank + SH], view("p1", rank), T.m[:, 0:512]).then_inc(S["q1"], 1)
     V.wait_ge(S["ldt"], 128)
-    V.tensor_scalar(T.bi[:], T.ltab[:, 4:12], -4096.0, -64.0, OP.mult, OP.add).then_inc(S["tb2"], 1)
-    V.tensor_scalar(T.o1[:], T.ltab[:, 0:4], 4.0, None, OP.mult).then_inc(S["tb1"], 1)
-    V.tensor_scalar(T.v2[:, 64:260:65], T.ltab[:, 4:8], 128.0, None, OP.add).then_inc(S["ba"], 1)
-    V.tensor_scalar(T.v3[:, 128:516:129], T.ltab[:, 8:12], 128.0, None, OP.add).then_inc(S["ba"], 1)
-    V.wait_ge(S["bc1"], 1)
-    V.tensor_tensor(T.kk[:, 0:CH], T.lb[:, 0:CH], T.pcs[:, 0:CH], OP.add).then_inc(S["kk1"], 1)
+    V.tensor_scalar(T.u4[:], T.ltab[:], 4.0, None, OP.mult).then_inc(S["u4"], 1)
+    V.tensor_scalar(T.bi[:], T.ltab[:, 4:12], -FAR, None, OP.mult).then_inc(S["bi"], 1)
+    V.wait_ge(S["ld1"], 16)
+    V.tensor_scalar(T.dq[:, 0:256], T.dlb[:, 0:256], 0.25, None, OP.mult).then_inc(S["dq1"], 1)
+    V.tensor_scalar(T.v2[:, 0:260:65], T.ltab[:, 4:8], -4.0, 508.0, OP.mult, OP.add).then_inc(S["ba"], 1)
 
     def make(t, off, *es):
-        lo = 256 * (RD - t)
+        hi = 256 + 256 * t
         for e in es:
-            V.tensor_tensor(T.m[:, lo - 256 + e:lo:4], T.m[:, lo + e:1280].indirect(off[:, 0:4]),
+            V.tensor_tensor(T.m[:, hi + e:hi + 256:4], T.m[:, e:hi].indirect(off[:, 0:4]),
                             T.dq[:, 256 * (t - 1) + e:256 * t:4], OP.add).then_inc(S["g%d" % t], 1)
 
-    V.wait_ge(S["tb1"], 1)
+    V.wait_ge(S["u4"], 1)
     V.wait_ge(S["dq1"], 1)
-    make(1, T.o1, 0, 1, 2)
-    V.wait_ge(S["bc2"], 1)
-    V.tensor_tensor(T.kk[:, CH:192], T.lb[:, CH:192], T.pcs[:, CH:192], OP.add).then_inc(S["kk2"], 1)
-    V.wait_ge(S["ba"], 2)
+    make(1, T.u4, 0, 1, 2)
+    V.wait_ge(S["rs"], 9)
+    V.wait_ge(S["vs"], 3)
+    V.tensor_tensor_scan(T.vm[:], T.rs[:], T.vs[:], T.ini[:], OP.add, OP.min).then_inc(S["vm"], 1)
+    V.wait_ge(S["ba"], 1)
     V.wait_ge(S["va"], 4)
-    V.tensor_tensor_scan(T.s2[:], T.r2[:], T.v2[:], 2 * LARGE, OP.add, OP.min).then_inc(S["s2"], 1)
-    make(1, T.o1, 3)
+    V.tensor_tensor_scan(T.s2[:], T.r2[:], T.v2[:], 0.0, OP.add, OP.min).then_inc(S["s2"], 1)
+    make(1, T.u4, 3)
     V.wait_ge(S["s2"], 1)
-    V.tensor_scalar(T.o2[:], T.s2[:, 64:260:65], 4.0, -256.0, OP.mult, OP.add).then_inc(S["o2"], 1)
-    V.wait_ge(S["vs"], 1)
-    V.tensor_tensor_scan(T.vm[:], T.vs[:], T.vs[:], 1.0e9, OP.min, OP.min).then_inc(S["vm"], 1)
+    V.tensor_scalar(T.o2[:], T.s2[:, 64:260:65], -1.0, 764.0, OP.mult, OP.add).then_inc(S["o2"], 1)
+    V.tensor_scalar(T.v3[:, 0:516:129], T.ltab[:, 8:12], -4.0, 508.0, OP.mult, OP.add).then_inc(S["vb"], 1)
     V.wait_ge(S["o2"], 1)
     V.wait_ge(S["g1"], 4)
     V.wait_ge(S["dq2"], 1)
-    V.wait_ge(S["vm"], 1)
-    V.tensor_scalar(T.sown[:], T.vm[:, CH - 1:192:CH], T.bas[:], None, OP.min).then_inc(S["own"], 1)
-    make(2, T.o2, 0, 1)
-    V.wait_ge(S["vb"], 4)
-    V.tensor_tensor_scan(T.s3[:], T.r3[:], T.v3[:], 2 * LARGE, OP.add, OP.min).then_inc(S["s3"], 1)
-    make(2, T.o2, 2)
-    V.wait_ge(S["s3"], 1)
-    V.tensor_scalar(T.o3[:], T.s3[:, 128:516:129], 4.0, None, OP.mult).then_inc(S["o3"], 1)
+    make(2, T.o2, 0, 1, 2)
+    V.wait_ge(S["vb"], 5)
+    V.tensor_tensor_scan(T.s3[:], T.r3[:], T.v3[:], 0.0, OP.add, OP.min).then_inc(S["s3"], 1)
     make(2, T.o2, 3)
+    V.wait_ge(S["s3"], 1)
+    V.tensor_scalar(T.o3[:], T.s3[:, 128:516:129], -1.0, 1020.0, OP.mult, OP.add).then_inc(S["o3"], 1)
     V.wait_ge(S["o3"], 1)
     V.wait_ge(S["dq3"], 1)
     V.wait_ge(S["g2"], 4)
     make(3, T.o3, 0, 1, 2, 3)
     V.wait_ge(S["g3"], 4)
-    V.quantize_mx(cdv, sdv, T.m[:, 0:768]).then_inc(S["qd"], 1)
-    V.wait_ge(S["ldx"], 16)
-    for t in range(RD):
+    V.quantize_mx(T.cd[:, 192 * rank:192 * rank + 192], view("p2", rank), T.m[:, 512:1280]).then_inc(S["q2"], 1)
+
+    def pack_x(t):
         V.quantize_mx(T.xq[:, SH * t:SH * t + SH], T.xs[:, SH * t:SH * t + SH], T.xb[:, 512 * t:512 * t + 512]).then_inc(S["qx%d" % t], 1)
+
+    V.wait_ge(S["ldx"], 16)
+    pack_x(0)
+    pack_x(1)
+    V.tensor_scalar(T.pc[:], T.pi[:], 3, 1, OP.logical_shift_right, OP.bitwise_and).then_inc(S["pab"], 1)
+    V.tensor_scalar(T.pg[:], T.pb[:], -96.0, None, OP.mult).then_inc(S["pf"], 1)
+    pack_x(2)
+    V.wait_ge(S["pab"], 2)
+    V.tensor_scalar(T.ph[:], T.pc[:], 3.0, None, OP.mult).then_inc(S["pf"], 1)
+    pack_x(3)
+    V.wait_ge(S["pf"], 2)
+    V.tensor_scalar(T.turn[:], T.six[:], T.pg[:], T.ph[:], OP.add, OP.add).then_inc(S["turn"], 1)
 
     def quarter(t):
         A.activation(T.dq[:, 256 * (t - 1):256 * t], T.dlb[:, 256 * (t - 1):256 * t], AF.Copy, scale=0.25).then_inc(S["dq%d" % t], 1)
 
-    A.wait_ge(S["ldd"], 16)
-    quarter(1)
-    A.wait_ge(S["tb2"], 1)
-    A.wait_ge(S["kk1"], 1)
+    def mark(out, n, value):
+        A.activation(out, T.zero[:, 0:n], AF.Identity, bias=float(value)).then_inc(S["rs"], 1)
+
+    A.wait_ge(S["rz"], 4)
+    mark(T.r2[:, 0:260:65], 4, LARGE)
+    mark(T.r3[:, 0:516:129], 4, LARGE)
+    for k in (0, 1):
+        mark(T.vs[:, CH + k:198:66], 3, FAR)
+    for t in (1, 2, 3):
+        for k in (0, 1) if t < 3 else (0,):
+            at = 66 * (t - 1) + CH + k
+            mark(T.rs[:, at:at + 1], 1, (256 - (SH + CH * t - 1)) * (1 - 2 * k))
+    A.wait_ge(S["num"], 1)
+    A.wait_ge(S["bis"], 1)
+    A.wait_ge(S["u4"], 1)
+    A.activation(T.lr[:], T.num[:].indirect(T.u4[:, 0:8]), AF.Copy).then_inc(S["lr"], 1)
+    A.activation(T.vs[:, 132:196], T.num[:].indirect(T.u4[:, 8:12]), AF.Abs, bias=T.bis[:], scale=FAR).then_inc(S["vs"], 1)
+    A.wait_ge(S["lr"], 1)
+    for t in (1, 2):
+        A.activation(T.vs[:, 66 * (t - 1):66 * (t - 1) + CH], T.lr[:, CH * (t - 1):CH * t], AF.Abs, bias=T.bis[:], scale=FAR).then_inc(S["vs"], 1)
+    A.wait_ge(S["bi"], 1)
     for s in range(4):
-        A.activation(T.v2[:, 65 * s:65 * s + CH], T.kk[:, 0:CH], AF.Abs, bias=T.bi[:, s:s + 1], scale=4096.0).then_inc(S["va"], 1)
+        A.activation(T.v2[:, 65 * s + 1:65 * s + 65], T.lr[:, 0:CH], AF.Abs, bias=T.bi[:, s:s + 1], scale=FAR).then_inc(S["va"], 1)
+    A.wait_ge(S["ld2"], 16)
     quarter(2)
-    A.wait_ge(S["kk2"], 1)
-    A.wait_ge(S["bis"], 2)
-    A.activation(T.vs[:], T.kk[:], AF.Abs, bias=T.bis[:], scale=4096.0).then_inc(S["vs"], 1)
+    A.wait_ge(S["vm"], 1)
+    A.activation(T.sown[:], T.vm[:, CH:198:66], AF.Copy, scale=-1.0).then_inc(S["own"], 1)
     for s in range(4):
-        A.activation(T.v3[:, 129 * s:129 * s + 128], T.kk[:, 0:128], AF.Abs, bias=T.bi[:, 4 + s:5 + s], scale=4096.0).then_inc(S["vb"], 1)
+        A.activation(T.v3[:, 129 * s + 1:129 * s + 129], T.lr[:], AF.Abs, bias=T.bi[:, 4 + s:5 + s], scale=FAR).then_inc(S["vb"], 1)
     quarter(3)
 
-    def bank(k, n):
-        return T.ps[:, 512 * k:512 * k + n]
+    pair = sorted((rank, mate))
+    groups = [("1", pair, "mate"), ("2", [rank], None), ("1", [twin], "twin"), ("2", [mate], "mate"),
+              ("1", [diag], "diag"), ("2", [twin], "twin"), ("2", [diag], "diag")]
+    number = {}
+    PE.wait_ge(S["q1"], 1)
+    PE.wait_ge(S["q2"], 1)
+    n = 0
+    for piece, ranks, who in groups:
+        if who:
+            landed(PE, "c" + piece, who)
+            landed(PE, "p" + piece, who)
+        for t in range(RD) if piece == "1" else (1, 2, 3):
+            if n < RD:
+                PE.wait_ge(S["qx%d" % t], 1)
+            if n >= 8:
+                PE.wait_ge(S["out%d" % (n - 8)], 2 if 0 < n - 8 < RD else 1)
+            if piece == "1":
+                c, s, lo, k = T.cb, T.sb, SH * ranks[0], SH * len(ranks)
+            else:
+                c, s, lo, k = T.cd, T.sd, 192 * ranks[0], max(SH, CH * t)
+            b = 512 * (n % 8)
+            PE.matmul_mx(T.ps[:, b:b + k], T.xq[:, SH * t:SH * t + SH], T.xs[:, SH * t:SH * t + SH], c[:, lo:lo + k], s[:, lo:lo + k],
+                         True, True).then_inc(S["made%d" % n], 1)
+            for q in ranks:
+                number[(piece, t, q)] = n
+            n += 1
 
-    def xt(t):
-        return T.xq[:, SH * t:SH * t + SH], T.xs[:, SH * t:SH * t + SH]
+    def move(E, out, in_):
+        return V.tensor_copy(out, in_) if E is V else A.activation(out, in_, AF.Copy)
 
-    PE.wait_ge(S["qb"], 1)
-    for q in near_r + far_r:
-        PE.wait_ge(S["base%d" % q], 2 * nb[q])
-    for t in range(RD):
-        PE.wait_ge(S["qx%d" % t], 1)
-        PE.matmul_mx(bank(t, 512), xt(t)[0], xt(t)[1], T.cb[:], T.sb[:], True, True).then_inc(S["pb%d" % t], 1)
-    banks = {(1, mine): 4, (2, mine): 5, (3, mine): 6, (1, other): 7, (2, other): 0, (3, other): 1}
-    first = {1: 128, 2: 64, 3: 0}
-
-    def changed(p):
-        for t in (1, 2, 3):
-            k = banks[(t, p)]
-            if k < RD:
-                PE.wait_ge(S["cb%d" % k], 1 if k == 0 else 2)
-            lo, hi = 384 * p + first[t], 384 * p + 384
-            PE.matmul_mx(bank(k, hi - lo), xt(t)[0], xt(t)[1], T.cd[:, lo:hi], T.sd[:, lo:hi], True, True).then_inc(S["pd%d%d" % (t, p)], 1)
-
-    PE.wait_ge(S["qd"], 1)
-    for q in near_r:
-        PE.wait_ge(S["chg%d" % q], 2 * nb[q])
-    changed(mine)
-    for q in far_r:
-        PE.wait_ge(S["chg%d" % q], 2 * nb[q])
-    changed(other)
-
-    def vcopy(out, in_):
-        return V.tensor_copy(out, in_)
-
-    def acopy(out, in_):
-        return A.activation(out, in_, AF.Copy)
-
-    def base_copy(q, cp, t):
-        q.wait_ge(S["pb%d" % t], 1)
+    def copy1(E, t, ranks):
+        n = number[("1", t, ranks[0])]
+        b = 512 * (n % 8)
+        E.wait_ge(S["made%d" % n], 1)
         if t == 0:
-            cp(T.yb[:, 0:512], bank(0, 512)).then_inc(S["cb0"], 1)
+            move(E, T.yb[:, SH * ranks[0]:SH * (ranks[-1] + 1)], T.ps[:, b:b + SH * len(ranks)]).then_inc(S["out%d" % n], 1)
             return
-        for p in (0, 1):
-            cp(T["w%d%d" % (t, p)][:, 384:640], T.ps[:, 512 * t + 256 * p:512 * t + 256 * p + 256]).then_inc(S["cb%d" % t], 1)
+        for i, q in enumerate(ranks):
+            move(E, T["w%d%d" % (t, q)][:, 0:SH], T.ps[:, b + SH * i:b + SH * i + SH]).then_inc(S["out%d" % n], 1)
 
-    def changed_copy(q, cp, t, p):
-        q.wait_ge(S["pd%d%d" % (t, p)], 1)
-        k, w, f = 512 * banks[(t, p)], T["w%d%d" % (t, p)], first[t]
-        if t > 1:
-            cp(w[:, f:384], T.ps[:, k:k + 384 - f]).then_inc(S["cd%d%d" % (t, p)], 1)
-            return
-        for h in (f, f + 192):
-            cp(w[:, h:h + CH], T.ps[:, k + h - f:k + h - f + CH]).then_inc(S["cd%d%d" % (t, p)], 1)
+    def copy2(E, t, q):
+        n = number[("2", t, q)]
+        b = 512 * (n % 8)
+        E.wait_ge(S["made%d" % n], 1)
+        move(E, T["w%d%d" % (t, q)][:, SH:SH + CH * t], T.ps[:, b:b + CH * t]).then_inc(S["out%d" % n], 1)
 
-    def order(t, p):
-        for h in (0, 1):
-            q = 2 * p + h
-            k = 8 * (4 * (t - 1) + q)
-            V.tensor_scalar(T.tabt[:, k:k + 8], T.tab[:, 3 * q + t - 1:96:12], -float(first[t]), None, OP.add).then_inc(S["tt%d%d" % (t, p)], 1)
+    def pick(E, t, q):
+        E.wait_ge(S["tt"], 1)
+        E.wait_ge(S["out%d" % number[("1", t, q)]], 2 if q in pair else 1)
+        E.wait_ge(S["out%d" % number[("2", t, q)]], 1)
+        k, c = 32 * (t - 1) + 8 * q, 512 * t + SH * q
+        move(E, T.yb[:, c:c + SH], T["w%d%d" % (t, q)][:].indirect(T.tabt[:, k:k + 8])).then_inc(S["ga%d%d" % (t, q)], 1)
 
-    def pick(q, cp, t, p, lo=0, hi=2):
-        q.wait_ge(S["tt%d%d" % (t, p)], 2)
-        q.wait_ge(S["cb%d" % t], 2)
-        q.wait_ge(S["cd%d%d" % (t, p)], 2 if t == 1 else 1)
-        k, c = 8 * (4 * (t - 1) + 2 * p), 512 * t + 256 * p
-        cp(T.yb[:, c + SH * lo:c + SH * hi],
-           T["w%d%d" % (t, p)][:, first[t]:640].indirect(T.tabt[:, k + 8 * lo:k + 8 * hi])).then_inc(S["ga%d%d" % (t, p)], hi - lo)
+    def rounds(E, q):
+        return (1, 2) if (E is A) == (q in (rank, twin)) else (3,)
 
-    base_copy(A, acopy, 0)
-    A.wait_ge(S["cb0"], 1)
-    A.dma_start(T.y[:, 0:512], T.yb[:, 0:512]).then_inc(S["st"], 16)
-    base_copy(A, acopy, 2)
-    changed_copy(A, acopy, 1, mine)
-    changed_copy(A, acopy, 2, mine)
-    pick(A, acopy, 1, mine)
-    pick(A, acopy, 2, mine)
-    changed_copy(A, acopy, 1, other)
-    pick(A, acopy, 1, other)
-    pick(A, acopy, 2, other, 1, 2)
-    pick(A, acopy, 3, other, 1, 2)
-    base_copy(V, vcopy, 1)
-    base_copy(V, vcopy, 3)
-    changed_copy(V, vcopy, 3, mine)
-    V.wait_ge(S["rep"], 128)
-    for t in (1, 2, 3):
-        order(t, mine)
-    pick(V, vcopy, 3, mine)
-    for t in (1, 2, 3):
-        order(t, other)
-    changed_copy(V, vcopy, 2, other)
-    changed_copy(V, vcopy, 3, other)
-    pick(V, vcopy, 2, other, 0, 1)
-    pick(V, vcopy, 3, other, 0, 1)
+    def finish(E, q):
+        for t in rounds(E, q):
+            copy2(E, t, q)
+            pick(E, t, q)
+
+    for E, ts in ((A, (0, 2)), (V, (1, 3))):
+        for t in ts:
+            copy1(E, t, pair)
+        for t in rounds(E, rank):
+            copy2(E, t, rank)
+        for t in ts:
+            copy1(E, t, [twin])
+        if E is V:
+            V.wait_ge(S["rep"], 64)
+            V.tensor_copy(T.tab[64:128, :], T.tab[0:64, :]).then_inc(S["dup"], 1)
+            V.wait_ge(S["dup"], 1)
+            V.wait_ge(S["turn"], 1)
+            V.tensor_scalar(T.tabt[:], T.tab[:].indirect(T.turn[:]), 256.0, None, OP.add).then_inc(S["tt"], 1)
+        for t in rounds(E, rank):
+            pick(E, t, rank)
+        finish(E, mate)
+        for t in ts:
+            copy1(E, t, [diag])
+        finish(E, twin)
+        finish(E, diag)
+
+    def store(t, ranks):
+        for q in ranks:
+            if t:
+                SY.wait_ge(S["ga%d%d" % (t, q)], 1)
+        if t == 0:
+            SY.wait_ge(S["out%d" % number[("1", 0, ranks[0])]], 1)
+        c, k = 512 * t + SH * ranks[0], SH * len(ranks)
+        SY.dma_start(T.y[:, c:c + k], T.yb[:, c:c + k]).then_inc(S["st"], 16)
 
     SY.wait_ge(S["own"], 1)
-    SY.dma_start(T.lst[:, 3 * rank:3 * rank + 3], T.sown[:]).then_inc(S["ownd"], 16)
+    SY.dma_start(slot, T.sown[:]).then_inc(S["ownd"], 16)
     SY.wait_ge(S["ownd"], 16)
-    for q in near_r + far_r:
-        SY.wait_ge(S["lst%d" % q], nb[q])
-    for k in range(8):
+    SY.wait_ge(S["lst"], 2 * len(far_e) + len(near_e))
+    for k in range(4):
         SY.dma_start(T.tab[16 * k:16 * k + 16, :], T.lst[:]).then_inc(S["rep"], 16)
-    for p, turn in ((mine, (1, 3, 2)), (other, (1, 2, 3))):
-        for t in turn:
-            SY.wait_ge(S["ga%d%d" % (t, p)], 2)
-            c = 512 * t + 256 * p
-            SY.dma_start(T.y[:, c:c + 256], T.yb[:, c:c + 256]).then_inc(S["st"], 16)
-    SY.wait_ge(S["st"], 16 * 7)
+    stores = [(0, pair), (0, [twin])] + [(t, pair) for t in (1, 3, 2)] + [(0, [diag])] + [(t, [q]) for q in (twin, diag) for t in (1, 3, 2)]
+    for t, ranks in stores:
+        store(t, ranks)
+    SY.wait_ge(S["st"], 16 * len(stores))

@@ -22,24 +22,20 @@ SCRATCH = {
     "zero": ("sbuf", [128, 4], "bfloat16"),
     "o2": ("sbuf", [128, 4], "uint16"),
     "o3": ("sbuf", [128, 4], "uint16"),
-    "pi": ("sbuf", [128, 1], "int32"),
-    "pb": ("sbuf", [128, 1], "int32"),
-    "pc": ("sbuf", [128, 1], "int32"),
-    "pg": ("sbuf", [128, 1], "float32"),
-    "ph": ("sbuf", [128, 1], "float32"),
-    "pj": ("sbuf", [128, 1], "float32"),
     "bis": ("sbuf", [128, 1], "float32"),
     "ini": ("sbuf", [128, 1], "float32"),
-    "sown": ("sbuf", [128, 3], "bfloat16"),
-    "lst": ("sbuf", [128, 12], "bfloat16"),
-    "tab": ("sbuf", [128, 96], "bfloat16"),
+    "lst": ("sbuf", [128, 24], "bfloat16"),
+    "tab": ("sbuf", [128, 128], "bfloat16"),
+    "tabx": ("sbuf", [128, 96], "bfloat16"),
+    "row": ("sbuf", [128, 32], "float32"),
+    "col": ("sbuf", [128, 32], "float32"),
     "six": ("sbuf", [128, 6], "float32"),
     "turn": ("sbuf", [128, 6], "uint16"),
     "tabt": ("sbuf", [128, 96], "uint16"),
-    "cb": ("sbuf", [128, 512], "float8_e4m3fn_x4"),
-    "sb": ("sbuf", [128, 512], "uint8"),
-    "cd": ("sbuf", [128, 768], "float8_e4m3fn_x4"),
-    "sd": ("sbuf", [128, 768], "uint8"),
+    "ca": ("sbuf", [128, 1024], "float8_e4m3fn_x4"),
+    "pa": ("sbuf", [128, 1024], "uint8"),
+    "cb": ("sbuf", [128, 320], "float8_e4m3fn_x4"),
+    "pb": ("sbuf", [128, 320], "uint8"),
     "xb": ("sbuf", [128, 2048], "bfloat16"),
     "xq": ("sbuf", [128, 512], "float8_e4m3fn_x4"),
     "xs": ("sbuf", [128, 512], "uint8"),
@@ -50,12 +46,15 @@ for _t in (1, 2, 3):
     for _q in range(4):
         SCRATCH["w%d%d" % (_t, _q)] = ("sbuf", [128, 128 + 64 * _t], "float32")
 
-PRODUCTS = 24
-SEMAPHORES = (["%s%s" % (piece, who) for piece in ("c1", "p1", "c2", "p2") for who in ("mate", "twin", "diag")]
-              + ["lst", "sent", "ldw", "ldt", "ld1", "ld2", "ldx", "iot", "nz", "num", "rz", "rs", "pab", "pf", "ini", "bis", "turn",
-                 "u4", "bi", "ba", "dq1", "dq2", "dq3", "q1", "q2", "lr", "va", "vb", "s2", "o2",
-                 "s3", "o3", "g1", "g2", "g3", "vs", "vm", "own", "ownd", "rep", "dup", "tt", "st"]
-              + ["qx%d" % t for t in range(4)]
+PRODUCTS = 22
+WHO = ("own", "mate", "twin", "diag")
+PIECES = ("c1", "p1", "c2", "p2", "c3", "p3")
+PLACE = {"1": (0, 256, 384, 768), "2": (128, 512, 640, 896), "3": (64, 128, 192, 256)}
+SEMAPHORES = (["%s%s" % (piece, who) for piece in PIECES for who in WHO[1:]]
+              + ["lst", "sent", "ldw", "ldt", "ld1", "ld2", "ldx", "ldy", "nz", "num", "rz", "rs", "ini", "bis", "row", "col", "turn", "pad",
+                 "u4", "bi", "ba", "dq1", "dq2", "dq3", "q1", "q2", "q3", "lr", "va", "vb", "s2", "o2",
+                 "s3", "o3", "g1", "g2", "g3", "vs", "vm", "own", "st"]
+              + ["qx%d" % t for t in range(4)] + ["t%d" % step for step in range(5)]
               + ["%s%d" % (n, j) for n in ("made", "out") for j in range(PRODUCTS)]
               + ["ga%d%d" % (t, q) for t in (1, 2, 3) for q in range(4)])
 
@@ -64,6 +63,7 @@ AF = ActivationFunctionType
 SH, CH, RD = 128, 64, 4
 LARGE = 2.0 ** 20
 FAR = 2048.0
+OWN, MATE, TWIN, DIAG = range(4)
 
 
 def rank_program(g, core, T, topo):
@@ -76,65 +76,75 @@ def rank_program(g, core, T, topo):
     mate_c = [c for c in peers if c in topo.cores_of(core)][0]
     twin_c = [c for c in peers if c != mate_c and topo.die(c) == topo.die(core)][0]
     diag_c = [c for c in peers if c not in (mate_c, twin_c)][0]
-    mate, twin, diag = T.rank_of(mate_c), T.rank_of(twin_c), T.rank_of(diag_c)
+    cores = [core, mate_c, twin_c, diag_c]
+    ranks = [T.rank_of(c) for c in cores]
     far_e = topo.engines(core, twin_c)
     chip_e = [e for e in topo.engines(core, mate_c) if e not in far_e]
     near_e = chip_e[0::2]
-    on_e = {"1": chip_e[1::2], "2": far_e}
+    engs = {(p, who): near_e if who == MATE else far_e for p in PIECES for who in (MATE, TWIN, DIAG)}
+    for p in ("c3", "p3"):
+        engs[(p, TWIN)], engs[(p, DIAG)] = far_e[0::2], far_e[1::2]
 
-    def transfer(cores, engs, sem, dst, src):
+    def transfer(to, es, sem, dsts, src):
         ids = []
-        for c in cores:
-            rid, pid = topo.addr(c, core)
+        for who in to:
+            rid, pid = topo.addr(cores[who], core)
             ids.append(DstId(rid=rid, pnc=pid))
-        return RemoteDMATransfer(dst_ids=ids, dma_engine_mask=sum(1 << e for e in engs), remote_sem=S[sem], srcs=[src], dsts=[dst] * len(cores))
+        return RemoteDMATransfer(dst_ids=ids, dma_engine_mask=sum(1 << e for e in es), remote_sem=S[sem], srcs=[src], dsts=dsts)
 
-    def view(piece, q):
-        if piece == "c1":
-            return T.cb[:, SH * q:SH * q + SH].bitcast(dt.uint8)
-        if piece == "p1":
-            return T.sb[:, SH * q:SH * q + SH]
-        if piece == "c2":
-            return T.cd[:, 192 * q:192 * q + 192].bitcast(dt.uint8)
-        return T.sd[:, 192 * q:192 * q + 192]
+    def view(piece, who):
+        kind, n = piece
+        lo = PLACE[n][who]
+        v = T[kind + ("b" if n == "3" else "a")][:, lo:lo + (CH if n == "3" else SH)]
+        return v.bitcast(dt.uint8) if kind == "c" else v
 
-    def send(piece):
-        v = view(piece, rank)
-        g.remote_dma_fused([transfer([twin_c], far_e, piece + "twin", v, v), transfer([mate_c], near_e, piece + "mate", v, v)], local_sem=S["sent"])
-        return len(far_e) + len(near_e)
+    def send(piece, to):
+        g.remote_dma_fused([transfer([who], engs[(piece, who)], piece + WHO[who], [view(piece, who)], view(piece, OWN)) for who in to],
+                           local_sem=S["sent"])
+        return sum(len(engs[(piece, who)]) for who in to)
 
     def landed(q, piece, who):
-        q.wait_ge(S[piece + who], len({"mate": near_e, "twin": far_e, "diag": on_e[piece[1]]}[who]))
+        q.wait_ge(S[piece + WHO[who]], len(engs[(piece, who)]))
 
     def hand_on(piece):
-        landed(g, piece, "twin")
-        v = view(piece, twin)
-        g.remote_dma_fused([transfer([mate_c], on_e[piece[1]], piece + "diag", v, v)], local_sem=S["sent"])
-        return len(on_e[piece[1]])
+        landed(g, piece, TWIN)
+        g.remote_dma_fused([transfer([MATE], engs[(piece, DIAG)], piece + "diag", [view(piece, DIAG)], view(piece, TWIN))], local_sem=S["sent"])
+        return len(engs[(piece, DIAG)])
 
     SY.dma_start(T.m[:, 0:512], T.wm[:]).then_inc(S["ldw"], 16)
     for k in range(8):
         (SY if k < 4 else A).dma_start(T.ltab[16 * k:16 * k + 16, :], T.idx[:]).then_inc(S["ldt"], 16)
     A.dma_start(T.dlb[:, 0:256], T.dl[:, 0:256]).then_inc(S["ld1"], 16)
     A.dma_start(T.dlb[:, 256:768], T.dl[:, 256:768]).then_inc(S["ld2"], 16)
-    SY.dma_start(T.xb[:], T.x[:]).then_inc(S["ldx"], 16)
+    SY.dma_start(T.xb[:, 1024:2048], T.x[:, 1024:2048]).then_inc(S["ldx"], 16)
+    SY.dma_start(T.xb[:, 0:1024], T.x[:, 0:1024]).then_inc(S["ldy"], 16)
 
-    g.iota(T.pi[:], [[0, 1]], 0, 1).then_inc(S["iot"], 1)
-    g.iota(T.pj[:], [[0, 1]], SH - 1, -16, allow_small_or_imprecise_dtypes=True).then_inc(S["iot"], 1)
-    g.iota(T.six[:], [[1, 3], [6, 2]], 0, 12, allow_small_or_imprecise_dtypes=True).then_inc(S["iot"], 1)
+    def iota(out, pattern, base, step, sem):
+        g.iota(out, pattern, base, step, allow_small_or_imprecise_dtypes=True).then_inc(S[sem], 1)
+
+    iota(T.ini[:], [[0, 1]], SH - 1, -1, "ini")
     g.wait_ge(S["nz"], 1)
-    g.iota(T.num[:, 0:512:4], [[1, SH]], 0, 0, allow_small_or_imprecise_dtypes=True).then_inc(S["num"], 1)
+    iota(T.num[:, 0:512:4], [[1, SH]], 0, 0, "num")
+    for up in (0, 1):
+        for h in (0, 1):
+            turned = up != h
+            iota(T.row[:, 16 * up + h:16 * up + 16:2], [[1, 2], [-32 if turned and up else 32, 2], [16, 2]], (64 + 32 * up) * turned, 0, "row")
+    iota(T.six[:], [[2, 6]], 0, 0, "row")
     sent = 0
     g.wait_ge(S["q1"], 1)
-    sent += send("c1")
+    sent += send("c1", (TWIN, MATE))
+    sent += send("p1", (TWIN, MATE))
     g.wait_ge(S["own"], 1)
-    slot = T.lst[:, 3 * rank:3 * rank + 3]
-    g.remote_dma_fused([transfer([twin_c, diag_c], far_e, "lst", slot, T.sown[:]), transfer([mate_c], near_e, "lst", slot, T.sown[:])], local_sem=S["sent"])
+    slot = [T.lst[:, 5 + 3 * who:8 + 3 * who] for who in range(4)]
+    g.remote_dma_fused([transfer([TWIN, DIAG], far_e, "lst", [slot[TWIN], slot[DIAG]], slot[OWN]),
+                        transfer([MATE], near_e, "lst", [slot[MATE]], slot[OWN])], local_sem=S["sent"])
     sent += len(far_e) + len(near_e)
-    sent += send("p1")
     g.wait_ge(S["q2"], 1)
-    sent += send("c2")
-    sent += send("p2")
+    sent += send("c2", (TWIN, MATE))
+    sent += send("p2", (TWIN, MATE))
+    g.wait_ge(S["q3"], 1)
+    sent += send("c3", (TWIN, DIAG, MATE))
+    sent += send("p3", (TWIN, DIAG, MATE))
     for piece in ("c1", "p1", "c2", "p2"):
         sent += hand_on(piece)
     g.wait_ge(S["sent"], sent)
@@ -143,15 +153,19 @@ def rank_program(g, core, T, topo):
     V.memset(T.r2[:], 4.0).then_inc(S["rz"], 1)
     V.memset(T.r3[:], 4.0).then_inc(S["rz"], 1)
     V.memset(T.zero[:], 0.0).then_inc(S["rz"], 1)
-    V.wait_ge(S["iot"], 3)
-    V.tensor_scalar(T.pb[:], T.pi[:], 3, None, OP.logical_shift_right).then_inc(S["pab"], 1)
     V.memset(T.rs[:], 1.0).then_inc(S["rz"], 1)
-    V.wait_ge(S["pab"], 1)
-    V.tensor_scalar(T.ini[:], T.pb[:], 127.0, T.pj[:], OP.mult, OP.add).then_inc(S["ini"], 1)
     V.wait_ge(S["ini"], 1)
     V.tensor_scalar(T.bis[:], T.ini[:], -127.0, FAR, OP.add, OP.mult).then_inc(S["bis"], 1)
+    V.memset(T.tab[0:32, 0:64], 0.0).then_inc(S["pad"], 1)
+
+    def pack(n, codes, plane, at, lo):
+        V.quantize_mx(codes[:, at:at + SH], plane[:, at:at + SH], T.m[:, lo:lo + 512]).then_inc(S["q%d" % n], 1)
+
+    def pack_x(t):
+        V.quantize_mx(T.xq[:, SH * t:SH * t + SH], T.xs[:, SH * t:SH * t + SH], T.xb[:, 512 * t:512 * t + 512]).then_inc(S["qx%d" % t], 1)
+
     V.wait_ge(S["ldw"], 16)
-    V.quantize_mx(T.cb[:, SH * rank:SH * rank + SH], view("p1", rank), T.m[:, 0:512]).then_inc(S["q1"], 1)
+    pack(1, T.ca, T.pa, 0, 0)
     V.wait_ge(S["ldt"], 128)
     V.tensor_scalar(T.u4[:], T.ltab[:], 4.0, None, OP.mult).then_inc(S["u4"], 1)
     V.tensor_scalar(T.bi[:], T.ltab[:, 4:12], -FAR, None, OP.mult).then_inc(S["bi"], 1)
@@ -181,33 +195,50 @@ def rank_program(g, core, T, topo):
     V.wait_ge(S["o2"], 1)
     V.wait_ge(S["g1"], 4)
     V.wait_ge(S["dq2"], 1)
-    make(2, T.o2, 0, 1, 2)
+    make(2, T.o2, 0, 1, 2, 3)
+    V.wait_ge(S["ldx"], 16)
+    pack_x(2)
+    V.wait_ge(S["g2"], 4)
+    pack(2, T.ca, T.pa, SH, 512)
+    pack_x(3)
     V.wait_ge(S["vb"], 5)
     V.tensor_tensor_scan(T.s3[:], T.r3[:], T.v3[:], 0.0, OP.add, OP.min).then_inc(S["s3"], 1)
-    make(2, T.o2, 3)
+    V.wait_ge(S["ldy"], 16)
+    pack_x(1)
     V.wait_ge(S["s3"], 1)
     V.tensor_scalar(T.o3[:], T.s3[:, 128:516:129], -1.0, 1020.0, OP.mult, OP.add).then_inc(S["o3"], 1)
+    pack_x(0)
     V.wait_ge(S["o3"], 1)
     V.wait_ge(S["dq3"], 1)
-    V.wait_ge(S["g2"], 4)
     make(3, T.o3, 0, 1, 2, 3)
+    V.wait_ge(S["row"], 5)
+    V.transpose(T.col[:], T.row[:]).then_inc(S["col"], 1)
     V.wait_ge(S["g3"], 4)
-    V.quantize_mx(T.cd[:, 192 * rank:192 * rank + 192], view("p2", rank), T.m[:, 512:1280]).then_inc(S["q2"], 1)
+    pack(3, T.cb, T.pb, 0, 768)
+    V.wait_ge(S["col"], 1)
+    V.tensor_scalar(T.turn[:], T.six[:], T.col[:, 0:1], None, OP.add).then_inc(S["turn"], 1)
 
-    def pack_x(t):
-        V.quantize_mx(T.xq[:, SH * t:SH * t + SH], T.xs[:, SH * t:SH * t + SH], T.xb[:, 512 * t:512 * t + 512]).then_inc(S["qx%d" % t], 1)
-
-    V.wait_ge(S["ldx"], 16)
-    pack_x(0)
-    pack_x(1)
-    V.tensor_scalar(T.pc[:], T.pi[:], 3, 1, OP.logical_shift_right, OP.bitwise_and).then_inc(S["pab"], 1)
-    V.tensor_scalar(T.pg[:], T.pb[:], -96.0, None, OP.mult).then_inc(S["pf"], 1)
-    pack_x(2)
-    V.wait_ge(S["pab"], 2)
-    V.tensor_scalar(T.ph[:], T.pc[:], 3.0, None, OP.mult).then_inc(S["pf"], 1)
-    pack_x(3)
-    V.wait_ge(S["pf"], 2)
-    V.tensor_scalar(T.turn[:], T.six[:], T.pg[:], T.ph[:], OP.add, OP.add).then_inc(S["turn"], 1)
+    def table(step):
+        done = S["t%d" % step]
+        if step == 0:
+            V.wait_ge(S["pad"], 1)
+            V.wait_ge(S["own"], 1)
+            V.wait_ge(S["lst"], 2 * len(far_e) + len(near_e))
+            for k in range(4):
+                V.tensor_copy(T.tab[0:32, 16 * k:16 * k + 12], T.lst[32 * k:32 * k + 32, 5:17]).then_inc(done, 1)
+            return
+        V.wait_ge(S["t%d" % (step - 1)], (4, 2, 1, 3)[step - 1])
+        if step == 1:
+            V.transpose(T.tabx[0:32, 0:64], T.tab[0:32, 0:64]).then_inc(done, 1)
+            V.transpose(T.tabx[0:32, 64:96], T.tab[0:32, 0:32]).then_inc(done, 1)
+        elif step == 2:
+            V.transpose(T.tab[0:32, 64:128], T.tabx[0:32, 16:80]).then_inc(done, 1)
+        elif step == 3:
+            for k in (1, 2, 3):
+                V.tensor_copy(T.tab[32 * k:32 * k + 32, :], T.tab[0:32, :]).then_inc(done, 1)
+        else:
+            V.wait_ge(S["turn"], 1)
+            V.tensor_scalar(T.tabt[:], T.tab[:].indirect(T.turn[:]), 256.0, None, OP.add).then_inc(done, 1)
 
     def quarter(t):
         A.activation(T.dq[:, 256 * (t - 1):256 * t], T.dlb[:, 256 * (t - 1):256 * t], AF.Copy, scale=0.25).then_inc(S["dq%d" % t], 1)
@@ -235,112 +266,99 @@ def rank_program(g, core, T, topo):
     A.wait_ge(S["bi"], 1)
     for s in range(4):
         A.activation(T.v2[:, 65 * s + 1:65 * s + 65], T.lr[:, 0:CH], AF.Abs, bias=T.bi[:, s:s + 1], scale=FAR).then_inc(S["va"], 1)
+    A.wait_ge(S["vm"], 1)
+    A.activation(slot[OWN], T.vm[:, CH:198:66], AF.Copy, scale=-1.0).then_inc(S["own"], 1)
     A.wait_ge(S["ld2"], 16)
     quarter(2)
-    A.wait_ge(S["vm"], 1)
-    A.activation(T.sown[:], T.vm[:, CH:198:66], AF.Copy, scale=-1.0).then_inc(S["own"], 1)
     for s in range(4):
         A.activation(T.v3[:, 129 * s + 1:129 * s + 129], T.lr[:], AF.Abs, bias=T.bi[:, 4 + s:5 + s], scale=FAR).then_inc(S["vb"], 1)
     quarter(3)
 
-    pair = sorted((rank, mate))
-    groups = [("1", pair, "mate"), ("2", [rank], None), ("1", [twin], "twin"), ("2", [mate], "mate"),
-              ("1", [diag], "diag"), ("2", [twin], "twin"), ("2", [diag], "diag")]
+    order = [("a", (OWN,), (2, 3, 1, 0)), ("b", (OWN,), (3,)), ("w", (MATE, TWIN), (0, 1, 2, 3)), ("d", (MATE, TWIN), (1, 2, 3)),
+             ("b", (MATE,), (3,)), ("w", (DIAG,), (0, 1, 2, 3)), ("b", (TWIN, DIAG), (3,)), ("d", (DIAG,), (3, 2, 1))]
     number = {}
-    PE.wait_ge(S["q1"], 1)
-    PE.wait_ge(S["q2"], 1)
     n = 0
-    for piece, ranks, who in groups:
-        if who:
-            landed(PE, "c" + piece, who)
-            landed(PE, "p" + piece, who)
-        for t in range(RD) if piece == "1" else (1, 2, 3):
+    for part, whos, ts in order:
+        for k in {"a": "12", "w": "1", "d": "2", "b": "3"}[part]:
+            for who in whos:
+                if who == OWN:
+                    PE.wait_ge(S["q" + k], 1)
+                else:
+                    landed(PE, "c" + k, who)
+                    landed(PE, "p" + k, who)
+        codes, plane = (T.cb, T.pb) if part == "b" else (T.ca, T.pa)
+        place = PLACE[{"a": "1", "w": "1", "d": "2", "b": "3"}[part]]
+        for t in ts:
             if n < RD:
                 PE.wait_ge(S["qx%d" % t], 1)
             if n >= 8:
-                PE.wait_ge(S["out%d" % (n - 8)], 2 if 0 < n - 8 < RD else 1)
-            if piece == "1":
-                c, s, lo, k = T.cb, T.sb, SH * ranks[0], SH * len(ranks)
-            else:
-                c, s, lo, k = T.cd, T.sd, 192 * ranks[0], max(SH, CH * t)
+                PE.wait_ge(S["out%d" % (n - 8)], len(number[n - 8]))
+            wide = {"a": SH + CH * min(t, 2), "w": SH, "d": CH * min(t, 2), "b": CH}[part]
+            lo, hi = place[whos[0]], place[whos[-1]] + wide
+            if hi - lo < SH:
+                lo, hi = (hi - SH, hi) if part == "b" else (lo, lo + SH)
             b = 512 * (n % 8)
-            PE.matmul_mx(T.ps[:, b:b + k], T.xq[:, SH * t:SH * t + SH], T.xs[:, SH * t:SH * t + SH], c[:, lo:lo + k], s[:, lo:lo + k],
-                         True, True).then_inc(S["made%d" % n], 1)
-            for q in ranks:
-                number[(piece, t, q)] = n
+            PE.matmul_mx(T.ps[:, b:b + hi - lo], T.xq[:, SH * t:SH * t + SH], T.xs[:, SH * t:SH * t + SH],
+                         codes[:, lo:hi], plane[:, lo:hi], True, True).then_inc(S["made%d" % n], 1)
+            number[n] = whos
+            for who in whos:
+                number[(part, t, who)] = (n, b + place[who] - lo, wide)
             n += 1
 
     def move(E, out, in_):
         return V.tensor_copy(out, in_) if E is V else A.activation(out, in_, AF.Copy)
 
-    def copy1(E, t, ranks):
-        n = number[("1", t, ranks[0])]
-        b = 512 * (n % 8)
+    def copy(E, part, t, first):
+        n = number[(part, t, first)][0]
         E.wait_ge(S["made%d" % n], 1)
-        if t == 0:
-            move(E, T.yb[:, SH * ranks[0]:SH * (ranks[-1] + 1)], T.ps[:, b:b + SH * len(ranks)]).then_inc(S["out%d" % n], 1)
-            return
-        for i, q in enumerate(ranks):
-            move(E, T["w%d%d" % (t, q)][:, 0:SH], T.ps[:, b + SH * i:b + SH * i + SH]).then_inc(S["out%d" % n], 1)
+        for who in number[n]:
+            _, b, k = number[(part, t, who)]
+            c = {"a": 0, "w": 0, "d": SH, "b": 2 * SH}[part]
+            out = T["w%d%d" % (t, who)][:, c:c + k] if t else T.yb[:, SH * ranks[who]:SH * ranks[who] + SH]
+            move(E, out, T.ps[:, b:b + k]).then_inc(S["out%d" % n], 1)
 
-    def copy2(E, t, q):
-        n = number[("2", t, q)]
-        b = 512 * (n % 8)
-        E.wait_ge(S["made%d" % n], 1)
-        move(E, T["w%d%d" % (t, q)][:, SH:SH + CH * t], T.ps[:, b:b + CH * t]).then_inc(S["out%d" % n], 1)
+    def copied(E, t, who):
+        for part in "awdb":
+            if (part, t, who) in number:
+                n = number[(part, t, who)][0]
+                E.wait_ge(S["out%d" % n], len(number[n]))
 
-    def pick(E, t, q):
-        E.wait_ge(S["tt"], 1)
-        E.wait_ge(S["out%d" % number[("1", t, q)]], 2 if q in pair else 1)
-        E.wait_ge(S["out%d" % number[("2", t, q)]], 1)
-        k, c = 32 * (t - 1) + 8 * q, 512 * t + SH * q
-        move(E, T.yb[:, c:c + SH], T["w%d%d" % (t, q)][:].indirect(T.tabt[:, k:k + 8])).then_inc(S["ga%d%d" % (t, q)], 1)
+    def pick(E, t, who):
+        E.wait_ge(S["t4"], 1)
+        copied(E, t, who)
+        k, c = 24 * who + 8 * (t - 1), 512 * t + SH * ranks[who]
+        move(E, T.yb[:, c:c + SH], T["w%d%d" % (t, who)][:].indirect(T.tabt[:, k:k + 8])).then_inc(S["ga%d%d" % (t, who)], 1)
 
-    def rounds(E, q):
-        return (1, 2) if (E is A) == (q in (rank, twin)) else (3,)
+    def steps(who, text):
+        return [(s[0], int(s[1]), who) for s in text.split()]
 
-    def finish(E, q):
-        for t in rounds(E, q):
-            copy2(E, t, q)
-            pick(E, t, q)
+    plan = {
+        A: steps(OWN, "a2 a3 a1 a0 b3") + steps(MATE, "w0 w1 w2 w3 d1 p1") + steps(TWIN, "p1") + steps(MATE, "d3 b3 p3")
+        + steps(DIAG, "w1 w3 d3 p3 p1"),
+        V: steps(OWN, "t0 t1 t2 t3 t4 p1 p2 p3") + steps(MATE, "d2 p2") + steps(TWIN, "p2") + steps(DIAG, "w0 w2")
+        + steps(TWIN, "b3 p3") + steps(DIAG, "d2 d1 p2"),
+    }
+    for E, todo in plan.items():
+        for kind, t, who in todo:
+            if kind == "t":
+                table(t)
+            elif kind == "p":
+                pick(E, t, who)
+            else:
+                copy(E, kind, t, who)
 
-    for E, ts in ((A, (0, 2)), (V, (1, 3))):
-        for t in ts:
-            copy1(E, t, pair)
-        for t in rounds(E, rank):
-            copy2(E, t, rank)
-        for t in ts:
-            copy1(E, t, [twin])
-        if E is V:
-            V.wait_ge(S["rep"], 64)
-            V.tensor_copy(T.tab[64:128, :], T.tab[0:64, :]).then_inc(S["dup"], 1)
-            V.wait_ge(S["dup"], 1)
-            V.wait_ge(S["turn"], 1)
-            V.tensor_scalar(T.tabt[:], T.tab[:].indirect(T.turn[:]), 256.0, None, OP.add).then_inc(S["tt"], 1)
-        for t in rounds(E, rank):
-            pick(E, t, rank)
-        finish(E, mate)
-        for t in ts:
-            copy1(E, t, [diag])
-        finish(E, twin)
-        finish(E, diag)
-
-    def store(t, ranks):
-        for q in ranks:
+    def store(t, whos):
+        for who in whos:
             if t:
-                SY.wait_ge(S["ga%d%d" % (t, q)], 1)
-        if t == 0:
-            SY.wait_ge(S["out%d" % number[("1", 0, ranks[0])]], 1)
-        c, k = 512 * t + SH * ranks[0], SH * len(ranks)
+                SY.wait_ge(S["ga%d%d" % (t, who)], 1)
+            else:
+                copied(SY, 0, who)
+        c, k = 512 * t + SH * min(ranks[who] for who in whos), SH * len(whos)
         SY.dma_start(T.y[:, c:c + k], T.yb[:, c:c + k]).then_inc(S["st"], 16)
 
-    SY.wait_ge(S["own"], 1)
-    SY.dma_start(slot, T.sown[:]).then_inc(S["ownd"], 16)
-    SY.wait_ge(S["ownd"], 16)
-    SY.wait_ge(S["lst"], 2 * len(far_e) + len(near_e))
-    for k in range(4):
-        SY.dma_start(T.tab[16 * k:16 * k + 16, :], T.lst[:]).then_inc(S["rep"], 16)
-    stores = [(0, pair), (0, [twin])] + [(t, pair) for t in (1, 3, 2)] + [(0, [diag])] + [(t, [q]) for q in (twin, diag) for t in (1, 3, 2)]
-    for t, ranks in stores:
-        store(t, ranks)
+    pair = (OWN, MATE)
+    stores = ([(0, pair), (0, (TWIN,)), (1, pair), (1, (TWIN,)), (2, pair), (2, (TWIN,)), (3, pair), (0, (DIAG,)), (3, (TWIN,))]
+              + [(t, (DIAG,)) for t in (3, 2, 1)])
+    for t, whos in stores:
+        store(t, whos)
     SY.wait_ge(S["st"], 16 * len(stores))

@@ -46,13 +46,21 @@ for _t in (1, 2, 3):
     for _q in range(4):
         SCRATCH["w%d%d" % (_t, _q)] = ("sbuf", [128, 128 + 64 * _t], "float32")
 
-PRODUCTS = 22
 WHO = ("own", "mate", "twin", "diag")
-PIECES = ("c1", "p1", "c2", "p2", "c3", "p3")
+PIECES = ("ls", "c1", "p1", "c2", "p2", "c3", "p3")
 PLACE = {"1": (0, 256, 384, 768), "2": (128, 512, 640, 896), "3": (64, 128, 192, 256)}
+LOADS = "w l0 l1 l2 l3 d1 x2 d2 x0", "l4 l5 l6 l7"
+CALLS = "c1tE p1tO+p1mn c1mN lstE+lsdO+lsmN c2tF+c2mN p2tF+p2mN c1hN c3tE+c3dO+c3mN p1hN p3tE+p3dO+p3mN c2hN p2hN"
+OWNER = "q1 u4 bi dq1 m10 m11 x2 m12 s2 m13 o2 vm m2 x1 q2 s3 x0 o3 x3 m3 q3"
+LISTS = "lr ba va vs dq2 own vb dq3"
+ORDER = "a1o a2o a0o a3o w0mt w1mt w3mt b3o w2mt d2mt d1mt d3mt w3d w1d b3m w0d d1d w2d b3td d3d d2d"
+PLAN_A = "a1o a2o a0o a3o w0m w1m w3m w2m d2m d1m p2t d3m w3d p3o p3m d1d w0d p1d p3t p2d"
+PLAN_V = "t0 t1 t2 t3 t4 b3o p1o p2m p2o w1d b3m p1t p1m w2d b3t d3d d2d p3d"
+STORES = "0p 0t 2t 2p 1t 3p 1p 0d 1d 3t 3d 2d"
+PRODUCTS = len(ORDER.split())
 SEMAPHORES = (["%s%s" % (piece, who) for piece in PIECES for who in WHO[1:]]
-              + ["lst", "sent", "ldw", "ldt", "ld1", "ld2", "ldx", "ldy", "nz", "num", "rz", "rs", "ini", "bis", "row", "col", "turn", "pad",
-                 "u4", "bi", "ba", "dq1", "dq2", "dq3", "q1", "q2", "q3", "lr", "va", "vb", "s2", "o2",
+              + ["sent", "ldw", "ldt", "ld1", "ld2", "ldx0", "ldx2", "nz", "num", "rz", "rs", "ini", "bis", "row", "col", "turn", "pad",
+                 "u4", "bi", "dq1", "dq2", "dq3", "q1", "q2", "q3", "lr", "va", "vb", "s2", "o2",
                  "s3", "o3", "g1", "g2", "g3", "vs", "vm", "own", "st"]
               + ["qx%d" % t for t in range(4)] + ["t%d" % step for step in range(5)]
               + ["%s%d" % (n, j) for n in ("made", "out") for j in range(PRODUCTS)]
@@ -80,74 +88,63 @@ def rank_program(g, core, T, topo):
     ranks = [T.rank_of(c) for c in cores]
     far_e = topo.engines(core, twin_c)
     chip_e = [e for e in topo.engines(core, mate_c) if e not in far_e]
-    near_e = chip_e[0::2]
-    engs = {(p, who): near_e if who == MATE else far_e for p in PIECES for who in (MATE, TWIN, DIAG)}
-    for p in ("c3", "p3"):
-        engs[(p, TWIN)], engs[(p, DIAG)] = far_e[0::2], far_e[1::2]
-
-    def transfer(to, es, sem, dsts, src):
-        ids = []
-        for who in to:
-            rid, pid = topo.addr(cores[who], core)
-            ids.append(DstId(rid=rid, pnc=pid))
-        return RemoteDMATransfer(dst_ids=ids, dma_engine_mask=sum(1 << e for e in es), remote_sem=S[sem], srcs=[src], dsts=dsts)
+    sets = {"F": far_e, "E": far_e[0::2], "O": far_e[1::2], "N": chip_e, "n": chip_e[0::2], "o": chip_e[1::2],
+            "M": far_e[1::2] + chip_e[0::2], "L": far_e[0::2] + chip_e[0::2]}
+    count = {(w[:2], "omtdh".index(w[2]) - (w[2] == "h")): len(sets[w[3]]) for call in CALLS.split() for w in call.split("+")}
 
     def view(piece, who):
+        if piece == "ls":
+            return T.lst[:, 5 + 3 * who:8 + 3 * who]
         kind, n = piece
         lo = PLACE[n][who]
         v = T[kind + ("b" if n == "3" else "a")][:, lo:lo + (CH if n == "3" else SH)]
         return v.bitcast(dt.uint8) if kind == "c" else v
 
-    def send(piece, to):
-        g.remote_dma_fused([transfer([who], engs[(piece, who)], piece + WHO[who], [view(piece, who)], view(piece, OWN)) for who in to],
-                           local_sem=S["sent"])
-        return sum(len(engs[(piece, who)]) for who in to)
-
     def landed(q, piece, who):
-        q.wait_ge(S[piece + WHO[who]], len(engs[(piece, who)]))
+        q.wait_ge(S[piece + WHO[who]], count[(piece, who)])
 
-    def hand_on(piece):
-        landed(g, piece, TWIN)
-        g.remote_dma_fused([transfer([MATE], engs[(piece, DIAG)], piece + "diag", [view(piece, DIAG)], view(piece, TWIN))], local_sem=S["sent"])
-        return len(engs[(piece, DIAG)])
+    def write(call):
+        transfers = []
+        for piece, to, es in [(w[:2], w[2], sets[w[3]]) for w in call.split("+")]:
+            if to == "h":
+                landed(g, piece, TWIN)
+                src, dst, who = TWIN, MATE, DIAG
+            else:
+                g.wait_ge(S["own" if piece == "ls" else "q" + piece[1]], 1)
+                src, dst, who = OWN, "omtd".index(to), "omtd".index(to)
+            rid, pid = topo.addr(cores[dst], core)
+            transfers.append(RemoteDMATransfer(dst_ids=[DstId(rid=rid, pnc=pid)], dma_engine_mask=sum(1 << e for e in es),
+                                               remote_sem=S[piece + WHO[who]], srcs=[view(piece, src)], dsts=[view(piece, who)]))
+        g.remote_dma_fused(transfers, local_sem=S["sent"])
 
-    SY.dma_start(T.m[:, 0:512], T.wm[:]).then_inc(S["ldw"], 16)
-    for k in range(8):
-        (SY if k < 4 else A).dma_start(T.ltab[16 * k:16 * k + 16, :], T.idx[:]).then_inc(S["ldt"], 16)
-    A.dma_start(T.dlb[:, 0:256], T.dl[:, 0:256]).then_inc(S["ld1"], 16)
-    A.dma_start(T.dlb[:, 256:768], T.dl[:, 256:768]).then_inc(S["ld2"], 16)
-    SY.dma_start(T.xb[:, 1024:2048], T.x[:, 1024:2048]).then_inc(S["ldx"], 16)
-    SY.dma_start(T.xb[:, 0:1024], T.x[:, 0:1024]).then_inc(S["ldy"], 16)
+    for q, names in zip((SY, A), LOADS):
+        for s in names.split():
+            if s[0] == "l":
+                k = 16 * int(s[1])
+                q.dma_start(T.ltab[k:k + 16, :], T.idx[:]).then_inc(S["ldt"], 16)
+            elif s == "w":
+                q.dma_start(T.m[:, 0:512], T.wm[:]).then_inc(S["ldw"], 16)
+            elif s[0] == "d":
+                lo, hi = (0, 256) if s == "d1" else (256, 768)
+                q.dma_start(T.dlb[:, lo:hi], T.dl[:, lo:hi]).then_inc(S["l" + s], 16)
+            else:
+                lo = 512 * int(s[1])
+                q.dma_start(T.xb[:, lo:lo + 1024], T.x[:, lo:lo + 1024]).then_inc(S["ld" + s], 16)
 
     def iota(out, pattern, base, step, sem):
         g.iota(out, pattern, base, step, allow_small_or_imprecise_dtypes=True).then_inc(S[sem], 1)
 
     iota(T.ini[:], [[0, 1]], SH - 1, -1, "ini")
-    g.wait_ge(S["nz"], 1)
-    iota(T.num[:, 0:512:4], [[1, SH]], 0, 0, "num")
     for up in (0, 1):
         for h in (0, 1):
             turned = up != h
             iota(T.row[:, 16 * up + h:16 * up + 16:2], [[1, 2], [-32 if turned and up else 32, 2], [16, 2]], (64 + 32 * up) * turned, 0, "row")
     iota(T.six[:], [[2, 6]], 0, 0, "row")
-    sent = 0
-    g.wait_ge(S["q1"], 1)
-    sent += send("c1", (TWIN, MATE))
-    sent += send("p1", (TWIN, MATE))
-    g.wait_ge(S["own"], 1)
-    slot = [T.lst[:, 5 + 3 * who:8 + 3 * who] for who in range(4)]
-    g.remote_dma_fused([transfer([TWIN, DIAG], far_e, "lst", [slot[TWIN], slot[DIAG]], slot[OWN]),
-                        transfer([MATE], near_e, "lst", [slot[MATE]], slot[OWN])], local_sem=S["sent"])
-    sent += len(far_e) + len(near_e)
-    g.wait_ge(S["q2"], 1)
-    sent += send("c2", (TWIN, MATE))
-    sent += send("p2", (TWIN, MATE))
-    g.wait_ge(S["q3"], 1)
-    sent += send("c3", (TWIN, DIAG, MATE))
-    sent += send("p3", (TWIN, DIAG, MATE))
-    for piece in ("c1", "p1", "c2", "p2"):
-        sent += hand_on(piece)
-    g.wait_ge(S["sent"], sent)
+    g.wait_ge(S["nz"], 1)
+    iota(T.num[:, 0:512:4], [[1, SH]], 0, 0, "num")
+    for call in CALLS.split():
+        write(call)
+    g.wait_ge(S["sent"], sum(count.values()))
 
     V.memset(T.num[:], 0.0).then_inc(S["nz"], 1)
     V.memset(T.r2[:], 4.0).then_inc(S["rz"], 1)
@@ -156,78 +153,77 @@ def rank_program(g, core, T, topo):
     V.memset(T.rs[:], 1.0).then_inc(S["rz"], 1)
     V.wait_ge(S["ini"], 1)
     V.tensor_scalar(T.bis[:], T.ini[:], -127.0, FAR, OP.add, OP.mult).then_inc(S["bis"], 1)
-    V.memset(T.tab[0:32, 0:64], 0.0).then_inc(S["pad"], 1)
-
-    def pack(n, codes, plane, at, lo):
-        V.quantize_mx(codes[:, at:at + SH], plane[:, at:at + SH], T.m[:, lo:lo + 512]).then_inc(S["q%d" % n], 1)
-
-    def pack_x(t):
-        V.quantize_mx(T.xq[:, SH * t:SH * t + SH], T.xs[:, SH * t:SH * t + SH], T.xb[:, 512 * t:512 * t + 512]).then_inc(S["qx%d" % t], 1)
-
-    V.wait_ge(S["ldw"], 16)
-    pack(1, T.ca, T.pa, 0, 0)
-    V.wait_ge(S["ldt"], 128)
-    V.tensor_scalar(T.u4[:], T.ltab[:], 4.0, None, OP.mult).then_inc(S["u4"], 1)
-    V.tensor_scalar(T.bi[:], T.ltab[:, 4:12], -FAR, None, OP.mult).then_inc(S["bi"], 1)
-    V.wait_ge(S["ld1"], 16)
-    V.tensor_scalar(T.dq[:, 0:256], T.dlb[:, 0:256], 0.25, None, OP.mult).then_inc(S["dq1"], 1)
-    V.tensor_scalar(T.v2[:, 0:260:65], T.ltab[:, 4:8], -4.0, 508.0, OP.mult, OP.add).then_inc(S["ba"], 1)
-
-    def make(t, off, *es):
-        hi = 256 + 256 * t
-        for e in es:
-            V.tensor_tensor(T.m[:, hi + e:hi + 256:4], T.m[:, e:hi].indirect(off[:, 0:4]),
-                            T.dq[:, 256 * (t - 1) + e:256 * t:4], OP.add).then_inc(S["g%d" % t], 1)
-
-    V.wait_ge(S["u4"], 1)
-    V.wait_ge(S["dq1"], 1)
-    make(1, T.u4, 0, 1, 2)
-    V.wait_ge(S["rs"], 9)
-    V.wait_ge(S["vs"], 3)
-    V.tensor_tensor_scan(T.vm[:], T.rs[:], T.vs[:], T.ini[:], OP.add, OP.min).then_inc(S["vm"], 1)
-    V.wait_ge(S["ba"], 1)
-    V.wait_ge(S["va"], 4)
-    V.tensor_tensor_scan(T.s2[:], T.r2[:], T.v2[:], 0.0, OP.add, OP.min).then_inc(S["s2"], 1)
-    make(1, T.u4, 3)
-    V.wait_ge(S["s2"], 1)
-    V.tensor_scalar(T.o2[:], T.s2[:, 64:260:65], -1.0, 764.0, OP.mult, OP.add).then_inc(S["o2"], 1)
-    V.tensor_scalar(T.v3[:, 0:516:129], T.ltab[:, 8:12], -4.0, 508.0, OP.mult, OP.add).then_inc(S["vb"], 1)
-    V.wait_ge(S["o2"], 1)
-    V.wait_ge(S["g1"], 4)
-    V.wait_ge(S["dq2"], 1)
-    make(2, T.o2, 0, 1, 2, 3)
-    V.wait_ge(S["ldx"], 16)
-    pack_x(2)
-    V.wait_ge(S["g2"], 4)
-    pack(2, T.ca, T.pa, SH, 512)
-    pack_x(3)
-    V.wait_ge(S["vb"], 5)
-    V.tensor_tensor_scan(T.s3[:], T.r3[:], T.v3[:], 0.0, OP.add, OP.min).then_inc(S["s3"], 1)
-    V.wait_ge(S["ldy"], 16)
-    pack_x(1)
-    V.wait_ge(S["s3"], 1)
-    V.tensor_scalar(T.o3[:], T.s3[:, 128:516:129], -1.0, 1020.0, OP.mult, OP.add).then_inc(S["o3"], 1)
-    pack_x(0)
-    V.wait_ge(S["o3"], 1)
-    V.wait_ge(S["dq3"], 1)
-    make(3, T.o3, 0, 1, 2, 3)
     V.wait_ge(S["row"], 5)
     V.transpose(T.col[:], T.row[:]).then_inc(S["col"], 1)
-    V.wait_ge(S["g3"], 4)
-    pack(3, T.cb, T.pb, 0, 768)
+    V.memset(T.tab[0:32, 0:64], 0.0).then_inc(S["pad"], 1)
     V.wait_ge(S["col"], 1)
     V.tensor_scalar(T.turn[:], T.six[:], T.col[:, 0:1], None, OP.add).then_inc(S["turn"], 1)
 
-    def table(step):
+    def quarter(E, t):
+        out, in_ = T.dq[:, 256 * (t - 1):256 * t], T.dlb[:, 256 * (t - 1):256 * t]
+        E.wait_ge(S["ld%d" % min(t, 2)], 16)
+        (V.tensor_scalar(out, in_, 0.25, None, OP.mult) if E is V else A.activation(out, in_, AF.Copy, scale=0.25)).then_inc(S["dq%d" % t], 1)
+
+    def owner(step):
+        if step == "u4":
+            V.wait_ge(S["ldt"], 128)
+            V.tensor_scalar(T.u4[:], T.ltab[:], 4.0, None, OP.mult).then_inc(S["u4"], 1)
+        elif step == "bi":
+            V.wait_ge(S["ldt"], 128)
+            V.tensor_scalar(T.bi[:], T.ltab[:, 4:12], -FAR, None, OP.mult).then_inc(S["bi"], 1)
+        elif step[0] == "d":
+            quarter(V, int(step[2]))
+        elif step == "vm":
+            V.wait_ge(S["rs"], 9)
+            V.wait_ge(S["vs"], 3)
+            V.tensor_tensor_scan(T.vm[:], T.rs[:], T.vs[:], T.ini[:], OP.add, OP.min).then_inc(S["vm"], 1)
+        elif step[0] == "s":
+            t = step[1]
+            V.wait_ge(S["rs"], 9)
+            V.wait_ge(S["va" if t == "2" else "vb"], 5)
+            V.tensor_tensor_scan(T["s" + t][:], T["r" + t][:], T["v" + t][:], 0.0, OP.add, OP.min).then_inc(S[step], 1)
+        elif step[0] == "o":
+            t = int(step[1])
+            k = CH * (t - 1)
+            V.wait_ge(S["s%d" % t], 1)
+            V.tensor_scalar(T[step][:], T["s%d" % t][:, k:4 * k + 4:k + 1], -1.0, 508.0 + 4 * k, OP.mult, OP.add).then_inc(S[step], 1)
+        elif step[0] == "m":
+            t = int(step[1])
+            off = "u4" if t == 1 else "o%d" % t
+            hi = 256 + 256 * t
+            V.wait_ge(S[off], 1)
+            V.wait_ge(S["dq%d" % t], 1)
+            V.wait_ge(S["g%d" % (t - 1) if t > 1 else "ldw"], 4 if t > 1 else 16)
+            for e in [int(e) for e in step[2:]] or range(4):
+                V.tensor_tensor(T.m[:, hi + e:hi + 256:4], T.m[:, e:hi].indirect(T[off][:, 0:4]),
+                                T.dq[:, 256 * (t - 1) + e:256 * t:4], OP.add).then_inc(S["g%d" % t], 1)
+        elif step[0] == "x":
+            t = int(step[1])
+            V.wait_ge(S["ldx%d" % (t - t % 2)], 16)
+            V.quantize_mx(T.xq[:, SH * t:SH * t + SH], T.xs[:, SH * t:SH * t + SH], T.xb[:, 512 * t:512 * t + 512]).then_inc(S["qx%d" % t], 1)
+        else:
+            n = int(step[1])
+            codes, plane, at, lo = ((T.ca, T.pa, 0, 0), (T.ca, T.pa, SH, 512), (T.cb, T.pb, 0, 768))[n - 1]
+            V.wait_ge(S["g%d" % n if n > 1 else "ldw"], 4 if n > 1 else 16)
+            V.quantize_mx(codes[:, at:at + SH], plane[:, at:at + SH], T.m[:, lo:lo + 512]).then_inc(S["q%d" % n], 1)
+
+    for step in OWNER.split():
+        owner(step)
+
+    def move(E, out, in_):
+        return V.tensor_copy(out, in_) if E is V else A.activation(out, in_, AF.Copy)
+
+    def table(E, step):
         done = S["t%d" % step]
         if step == 0:
-            V.wait_ge(S["pad"], 1)
-            V.wait_ge(S["own"], 1)
-            V.wait_ge(S["lst"], 2 * len(far_e) + len(near_e))
+            E.wait_ge(S["pad"], 1)
+            E.wait_ge(S["own"], 1)
+            for who in (MATE, TWIN, DIAG):
+                landed(E, "ls", who)
             for k in range(4):
-                V.tensor_copy(T.tab[0:32, 16 * k:16 * k + 12], T.lst[32 * k:32 * k + 32, 5:17]).then_inc(done, 1)
+                move(E, T.tab[0:32, 16 * k:16 * k + 12], T.lst[32 * k:32 * k + 32, 5:17]).then_inc(done, 1)
             return
-        V.wait_ge(S["t%d" % (step - 1)], (4, 2, 1, 3)[step - 1])
+        E.wait_ge(S["t%d" % (step - 1)], (4, 2, 1, 3)[step - 1])
         if step == 1:
             V.transpose(T.tabx[0:32, 0:64], T.tab[0:32, 0:64]).then_inc(done, 1)
             V.transpose(T.tabx[0:32, 64:96], T.tab[0:32, 0:32]).then_inc(done, 1)
@@ -235,16 +231,16 @@ def rank_program(g, core, T, topo):
             V.transpose(T.tab[0:32, 64:128], T.tabx[0:32, 16:80]).then_inc(done, 1)
         elif step == 3:
             for k in (1, 2, 3):
-                V.tensor_copy(T.tab[32 * k:32 * k + 32, :], T.tab[0:32, :]).then_inc(done, 1)
+                move(E, T.tab[32 * k:32 * k + 32, :], T.tab[0:32, :]).then_inc(done, 1)
         else:
             V.wait_ge(S["turn"], 1)
             V.tensor_scalar(T.tabt[:], T.tab[:].indirect(T.turn[:]), 256.0, None, OP.add).then_inc(done, 1)
 
-    def quarter(t):
-        A.activation(T.dq[:, 256 * (t - 1):256 * t], T.dlb[:, 256 * (t - 1):256 * t], AF.Copy, scale=0.25).then_inc(S["dq%d" % t], 1)
-
     def mark(out, n, value):
         A.activation(out, T.zero[:, 0:n], AF.Identity, bias=float(value)).then_inc(S["rs"], 1)
+
+    def compare(out, entries, bias, sem):
+        A.activation(out, entries, AF.Abs, bias=bias, scale=FAR).then_inc(S[sem], 1)
 
     A.wait_ge(S["rz"], 4)
     mark(T.r2[:, 0:260:65], 4, LARGE)
@@ -257,56 +253,71 @@ def rank_program(g, core, T, topo):
             mark(T.rs[:, at:at + 1], 1, (256 - (SH + CH * t - 1)) * (1 - 2 * k))
     A.wait_ge(S["num"], 1)
     A.wait_ge(S["bis"], 1)
-    A.wait_ge(S["u4"], 1)
-    A.activation(T.lr[:], T.num[:].indirect(T.u4[:, 0:8]), AF.Copy).then_inc(S["lr"], 1)
-    A.activation(T.vs[:, 132:196], T.num[:].indirect(T.u4[:, 8:12]), AF.Abs, bias=T.bis[:], scale=FAR).then_inc(S["vs"], 1)
-    A.wait_ge(S["lr"], 1)
-    for t in (1, 2):
-        A.activation(T.vs[:, 66 * (t - 1):66 * (t - 1) + CH], T.lr[:, CH * (t - 1):CH * t], AF.Abs, bias=T.bis[:], scale=FAR).then_inc(S["vs"], 1)
-    A.wait_ge(S["bi"], 1)
-    for s in range(4):
-        A.activation(T.v2[:, 65 * s + 1:65 * s + 65], T.lr[:, 0:CH], AF.Abs, bias=T.bi[:, s:s + 1], scale=FAR).then_inc(S["va"], 1)
-    A.wait_ge(S["vm"], 1)
-    A.activation(slot[OWN], T.vm[:, CH:198:66], AF.Copy, scale=-1.0).then_inc(S["own"], 1)
-    A.wait_ge(S["ld2"], 16)
-    quarter(2)
-    for s in range(4):
-        A.activation(T.v3[:, 129 * s + 1:129 * s + 129], T.lr[:], AF.Abs, bias=T.bi[:, 4 + s:5 + s], scale=FAR).then_inc(S["vb"], 1)
-    quarter(3)
 
-    order = [("a", (OWN,), (2, 3, 1, 0)), ("b", (OWN,), (3,)), ("w", (MATE, TWIN), (0, 1, 2, 3)), ("d", (MATE, TWIN), (1, 2, 3)),
-             ("b", (MATE,), (3,)), ("w", (DIAG,), (0, 1, 2, 3)), ("b", (TWIN, DIAG), (3,)), ("d", (DIAG,), (3, 2, 1))]
+    def lists(step):
+        if step == "lr":
+            A.wait_ge(S["u4"], 1)
+            A.activation(T.lr[:], T.num[:].indirect(T.u4[:, 0:8]), AF.Copy).then_inc(S["lr"], 1)
+        elif step == "vs":
+            A.wait_ge(S["u4"], 1)
+            compare(T.vs[:, 132:196], T.num[:].indirect(T.u4[:, 8:12]), T.bis[:], "vs")
+            A.wait_ge(S["lr"], 1)
+            for t in (1, 2):
+                compare(T.vs[:, 66 * (t - 1):66 * (t - 1) + CH], T.lr[:, CH * (t - 1):CH * t], T.bis[:], "vs")
+        elif step == "ba":
+            A.wait_ge(S["bi"], 1)
+            A.activation(T.v2[:, 0:260:65], T.bi[:, 0:4], AF.Identity, bias=508.0, scale=4 / FAR).then_inc(S["va"], 1)
+        elif step == "va":
+            A.wait_ge(S["bi"], 1)
+            A.wait_ge(S["lr"], 1)
+            for s in range(4):
+                compare(T.v2[:, 65 * s + 1:65 * s + 65], T.lr[:, 0:CH], T.bi[:, s:s + 1], "va")
+        elif step == "vb":
+            A.wait_ge(S["bi"], 1)
+            A.wait_ge(S["lr"], 1)
+            A.activation(T.v3[:, 0:516:129], T.bi[:, 4:8], AF.Identity, bias=508.0, scale=4 / FAR).then_inc(S["vb"], 1)
+            for s in range(4):
+                compare(T.v3[:, 129 * s + 1:129 * s + 129], T.lr[:], T.bi[:, 4 + s:5 + s], "vb")
+        elif step == "own":
+            A.wait_ge(S["vm"], 1)
+            A.activation(view("ls", OWN), T.vm[:, CH:198:66], AF.Copy, scale=-1.0).then_inc(S["own"], 1)
+        else:
+            quarter(A, int(step[2]))
+
+    for step in LISTS.split():
+        lists(step)
+
     number = {}
-    n = 0
-    for part, whos, ts in order:
-        for k in {"a": "12", "w": "1", "d": "2", "b": "3"}[part]:
-            for who in whos:
-                if who == OWN:
-                    PE.wait_ge(S["q" + k], 1)
-                else:
-                    landed(PE, "c" + k, who)
-                    landed(PE, "p" + k, who)
+    seen = set()
+    for n, s in enumerate(ORDER.split()):
+        part, t, whos = s[0], int(s[1]), ["omtd".index(w) for w in s[2:]]
         codes, plane = (T.cb, T.pb) if part == "b" else (T.ca, T.pa)
         place = PLACE[{"a": "1", "w": "1", "d": "2", "b": "3"}[part]]
-        for t in ts:
-            if n < RD:
-                PE.wait_ge(S["qx%d" % t], 1)
-            if n >= 8:
-                PE.wait_ge(S["out%d" % (n - 8)], len(number[n - 8]))
-            wide = {"a": SH + CH * min(t, 2), "w": SH, "d": CH * min(t, 2), "b": CH}[part]
-            lo, hi = place[whos[0]], place[whos[-1]] + wide
-            if hi - lo < SH:
-                lo, hi = (hi - SH, hi) if part == "b" else (lo, lo + SH)
-            b = 512 * (n % 8)
-            PE.matmul_mx(T.ps[:, b:b + hi - lo], T.xq[:, SH * t:SH * t + SH], T.xs[:, SH * t:SH * t + SH],
-                         codes[:, lo:hi], plane[:, lo:hi], True, True).then_inc(S["made%d" % n], 1)
-            number[n] = whos
-            for who in whos:
-                number[(part, t, who)] = (n, b + place[who] - lo, wide)
-            n += 1
-
-    def move(E, out, in_):
-        return V.tensor_copy(out, in_) if E is V else A.activation(out, in_, AF.Copy)
+        wide = {"a": SH + CH * min(t, 2), "w": SH, "d": CH * min(t, 2), "b": CH}[part]
+        lo, hi = place[whos[0]], place[whos[-1]] + wide
+        short = hi - lo < SH
+        if short:
+            lo, hi = (hi - SH, hi) if part == "b" else (lo, lo + SH)
+        for k in {"a": "12" if t else "1", "w": "1", "d": "2", "b": "3"}[part]:
+            for who in [max(whos[0] - (short and part == "b"), OWN)] + whos:
+                if (k, who) not in seen:
+                    seen.add((k, who))
+                    if who == OWN:
+                        PE.wait_ge(S["q" + k], 1)
+                    else:
+                        landed(PE, "c" + k, who)
+                        landed(PE, "p" + k, who)
+        if t not in seen:
+            seen.add(t)
+            PE.wait_ge(S["qx%d" % t], 1)
+        if n >= 8:
+            PE.wait_ge(S["out%d" % (n - 8)], len(number[n - 8]))
+        b = 512 * (n % 8)
+        PE.matmul_mx(T.ps[:, b:b + hi - lo], T.xq[:, SH * t:SH * t + SH], T.xs[:, SH * t:SH * t + SH],
+                     codes[:, lo:hi], plane[:, lo:hi], True, True).then_inc(S["made%d" % n], 1)
+        number[n] = whos
+        for who in whos:
+            number[(part, t, who)] = (n, b + place[who] - lo, wide)
 
     def copy(E, part, t, first):
         n = number[(part, t, first)][0]
@@ -329,36 +340,30 @@ def rank_program(g, core, T, topo):
         k, c = 24 * who + 8 * (t - 1), 512 * t + SH * ranks[who]
         move(E, T.yb[:, c:c + SH], T["w%d%d" % (t, who)][:].indirect(T.tabt[:, k:k + 8])).then_inc(S["ga%d%d" % (t, who)], 1)
 
-    def steps(who, text):
-        return [(s[0], int(s[1]), who) for s in text.split()]
-
-    plan = {
-        A: steps(OWN, "a2 a3 a1 a0 b3") + steps(MATE, "w0 w1 w2 w3 d1 p1") + steps(TWIN, "p1") + steps(MATE, "d3 b3 p3")
-        + steps(DIAG, "w1 w3 d3 p3 p1"),
-        V: steps(OWN, "t0 t1 t2 t3 t4 p1 p2 p3") + steps(MATE, "d2 p2") + steps(TWIN, "p2") + steps(DIAG, "w0 w2")
-        + steps(TWIN, "b3 p3") + steps(DIAG, "d2 d1 p2"),
-    }
-    for E, todo in plan.items():
-        for kind, t, who in todo:
-            if kind == "t":
-                table(t)
-            elif kind == "p":
-                pick(E, t, who)
-            else:
-                copy(E, kind, t, who)
-
-    def store(t, whos):
+    def store(q, t, whos):
         for who in whos:
             if t:
-                SY.wait_ge(S["ga%d%d" % (t, who)], 1)
+                q.wait_ge(S["ga%d%d" % (t, who)], 1)
             else:
-                copied(SY, 0, who)
+                copied(q, 0, who)
         c, k = 512 * t + SH * min(ranks[who] for who in whos), SH * len(whos)
-        SY.dma_start(T.y[:, c:c + k], T.yb[:, c:c + k]).then_inc(S["st"], 16)
+        q.dma_start(T.y[:, c:c + k], T.yb[:, c:c + k]).then_inc(S["st"], 16)
 
-    pair = (OWN, MATE)
-    stores = ([(0, pair), (0, (TWIN,)), (1, pair), (1, (TWIN,)), (2, pair), (2, (TWIN,)), (3, pair), (0, (DIAG,)), (3, (TWIN,))]
-              + [(t, (DIAG,)) for t in (3, 2, 1)])
-    for t, whos in stores:
-        store(t, whos)
-    SY.wait_ge(S["st"], 16 * len(stores))
+    blocks = {"p": (OWN, MATE), "f": (TWIN, DIAG), "o": (OWN,), "m": (MATE,), "t": (TWIN,), "d": (DIAG,)}
+
+    for E, todo in ((A, PLAN_A), (V, PLAN_V)):
+        for s in todo.split():
+            if s[0] == "t":
+                table(E, int(s[1]))
+            elif s[0] == "p":
+                pick(E, int(s[1]), "omtd".index(s[2]))
+            elif s[0] == "x":
+                owner(s)
+            elif s[0] == "s":
+                store(A, int(s[1]), blocks[s[2]])
+            else:
+                copy(E, s[0], int(s[1]), "omtd".index(s[2]))
+
+    for s in STORES.split():
+        store(SY, int(s[0]), blocks[s[1]])
+    SY.wait_ge(S["st"], 16 * (len(STORES.split()) + sum(s[0] == "s" for s in PLAN_A.split())))

from concourse.bass import DstId, RemoteDMATransfer
from concourse.mybir import dt, AluOpType, AxisListType, ActivationFunctionType

SCRATCH = {
    "m": ("sbuf", [128, 1280], "bfloat16"),
    "dlb": ("sbuf", [128, 768], "bfloat16"),
    "dq": ("sbuf", [128, 768], "bfloat16"),
    "ltab": ("sbuf", [128, 12], "int32"),
    "u4": ("sbuf", [128, 12], "uint16"),
    "num": ("sbuf", [128, 512], "bfloat16"),
    "lr": ("sbuf", [128, 128], "float32"),
    "bi": ("sbuf", [128, 8], "float32"),
    "v2": ("sbuf", [128, 260], "bfloat16"),
    "v3": ("sbuf", [128, 516], "bfloat16"),
    "r2": ("sbuf", [128, 260], "bfloat16"),
    "r3": ("sbuf", [128, 516], "bfloat16"),
    "s2": ("sbuf", [128, 260], "bfloat16"),
    "s3": ("sbuf", [128, 516], "bfloat16"),
    "vs": ("sbuf", [128, 198], "bfloat16"),
    "rs": ("sbuf", [128, 198], "bfloat16"),
    "vm": ("sbuf", [128, 198], "bfloat16"),
    "zero": ("sbuf", [128, 4], "bfloat16"),
    "o2": ("sbuf", [128, 4], "uint16"),
    "o3": ("sbuf", [128, 4], "uint16"),
    "bis": ("sbuf", [128, 1], "float32"),
    "ini": ("sbuf", [128, 1], "float32"),
    "lst": ("sbuf", [128, 24], "bfloat16"),
    "tab": ("sbuf", [128, 128], "bfloat16"),
    "tabx": ("sbuf", [128, 96], "bfloat16"),
    "row": ("sbuf", [128, 32], "float32"),
    "col": ("sbuf", [128, 32], "float32"),
    "six": ("sbuf", [128, 6], "float32"),
    "turn": ("sbuf", [128, 6], "uint16"),
    "tabt": ("sbuf", [128, 96], "uint16"),
    "ca": ("sbuf", [128, 1024], "float8_e4m3fn_x4"),
    "pa": ("sbuf", [128, 1024], "uint8"),
    "cb": ("sbuf", [128, 320], "float8_e4m3fn_x4"),
    "pb": ("sbuf", [128, 320], "uint8"),
    "xb": ("sbuf", [128, 2048], "bfloat16"),
    "xq": ("sbuf", [128, 512], "float8_e4m3fn_x4"),
    "xs": ("sbuf", [128, 512], "uint8"),
    "yb": ("sbuf", [128, 2048], "float32"),
    "ps": ("psum", [128, 4096], "float32"),
}
for _t in (1, 2, 3):
    for _q in range(4):
        SCRATCH["w%d%d" % (_t, _q)] = ("sbuf", [128, 128 + 64 * _t], "float32")

WHO = ("own", "mate", "twin", "diag")
PIECES = ("ls", "c1", "p1", "c2", "p2", "c3", "p3")
PLACE = {"1": (0, 256, 384, 768), "2": (128, 512, 640, 896), "3": (64, 128, 192, 256)}
LOADS = "w l0 l1 l2 l3 d1 x2 d2 x0", "l4 l5 l6 l7"
CALLS = "c1tE p1tO+p1mn c1mN lstE+lsdO+lsmN c2tF+c2mN p2tF+p2mN c1hN c3tE+c3dO+c3mN p1hN p3tE+p3dO+p3mN c2hN p2hN"
OWNER = "q1 u4 bi dq1 m10 m11 x2 m12 s2 m13 o2 vm m2 x1 q2 s3 x0 o3 x3 m3 q3"
LISTS = "lr ba va vs dq2 own vb dq3"
ORDER = "a1o a2o a0o a3o w0mt w1mt w3mt b3o w2mt d2mt d1mt d3mt w3d w1d b3m w0d d1d w2d b3td d3d d2d"
PLAN_A = "a1o a2o a0o a3o w0m w1m w3m w2m d2m d1m p2t d3m w3d p3o p3m d1d w0d p1d p3t p2d"
PLAN_V = "t0 t1 t2 t3 t4 b3o p1o p2m p2o w1d b3m p1t p1m w2d b3t d3d d2d p3d"
STORES = "0p 0t 2t 2p 1t 3p 1p 0d 1d 3t 3d 2d"
PRODUCTS = len(ORDER.split())
SEMAPHORES = (["%s%s" % (piece, who) for piece in PIECES for who in WHO[1:]]
              + ["sent", "ldw", "ldt", "ld1", "ld2", "ldx0", "ldx2", "nz", "num", "rz", "rs", "ini", "bis", "row", "col", "turn", "pad",
                 "u4", "bi", "dq1", "dq2", "dq3", "q1", "q2", "q3", "lr", "va", "vb", "s2", "o2",
                 "s3", "o3", "g1", "g2", "g3", "vs", "vm", "own", "st"]
              + ["qx%d" % t for t in range(4)] + ["t%d" % step for step in range(5)]
              + ["%s%d" % (n, j) for n in ("made", "out") for j in range(PRODUCTS)]
              + ["ga%d%d" % (t, q) for t in (1, 2, 3) for q in range(4)])

OP = AluOpType
AF = ActivationFunctionType
SH, CH, RD = 128, 64, 4
LARGE = 2.0 ** 20
FAR = 2048.0
OWN, MATE, TWIN, DIAG = range(4)


def rank_program(g, core, T, topo):
    rank = T.rank_of(core)
    if rank is None:
        return
    S = T.sem
    V, A, PE, SY = g.vector, g.scalar, g.tensor, g.sync
    peers = [c for c in T.cores if c != core]
    mate_c = [c for c in peers if c in topo.cores_of(core)][0]
    twin_c = [c for c in peers if c != mate_c and topo.die(c) == topo.die(core)][0]
    diag_c = [c for c in peers if c not in (mate_c, twin_c)][0]
    cores = [core, mate_c, twin_c, diag_c]
    ranks = [T.rank_of(c) for c in cores]
    far_e = topo.engines(core, twin_c)
    chip_e = [e for e in topo.engines(core, mate_c) if e not in far_e]
    sets = {"F": far_e, "E": far_e[0::2], "O": far_e[1::2], "N": chip_e, "n": chip_e[0::2], "o": chip_e[1::2],
            "M": far_e[1::2] + chip_e[0::2], "L": far_e[0::2] + chip_e[0::2]}
    count = {(w[:2], "omtdh".index(w[2]) - (w[2] == "h")): len(sets[w[3]]) for call in CALLS.split() for w in call.split("+")}

    def view(piece, who):
        if piece == "ls":
            return T.lst[:, 5 + 3 * who:8 + 3 * who]
        kind, n = piece
        lo = PLACE[n][who]
        v = T[kind + ("b" if n == "3" else "a")][:, lo:lo + (CH if n == "3" else SH)]
        return v.bitcast(dt.uint8) if kind == "c" else v

    def landed(q, piece, who):
        q.wait_ge(S[piece + WHO[who]], count[(piece, who)])

    def write(call):
        transfers = []
        for piece, to, es in [(w[:2], w[2], sets[w[3]]) for w in call.split("+")]:
            if to == "h":
                landed(g, piece, TWIN)
                src, dst, who = TWIN, MATE, DIAG
            else:
                g.wait_ge(S["own" if piece == "ls" else "q" + piece[1]], 1)
                src, dst, who = OWN, "omtd".index(to), "omtd".index(to)
            rid, pid = topo.addr(cores[dst], core)
            transfers.append(RemoteDMATransfer(dst_ids=[DstId(rid=rid, pnc=pid)], dma_engine_mask=sum(1 << e for e in es),
                                               remote_sem=S[piece + WHO[who]], srcs=[view(piece, src)], dsts=[view(piece, who)]))
        g.remote_dma_fused(transfers, local_sem=S["sent"])

    for q, names in zip((SY, A), LOADS):
        for s in names.split():
            if s[0] == "l":
                k = 16 * int(s[1])
                q.dma_start(T.ltab[k:k + 16, :], T.idx[:]).then_inc(S["ldt"], 16)
            elif s == "w":
                q.dma_start(T.m[:, 0:512], T.wm[:]).then_inc(S["ldw"], 16)
            elif s[0] == "d":
                lo, hi = (0, 256) if s == "d1" else (256, 768)
                q.dma_start(T.dlb[:, lo:hi], T.dl[:, lo:hi]).then_inc(S["l" + s], 16)
            else:
                lo = 512 * int(s[1])
                q.dma_start(T.xb[:, lo:lo + 1024], T.x[:, lo:lo + 1024]).then_inc(S["ld" + s], 16)

    def iota(out, pattern, base, step, sem):
        g.iota(out, pattern, base, step, allow_small_or_imprecise_dtypes=True).then_inc(S[sem], 1)

    iota(T.ini[:], [[0, 1]], SH - 1, -1, "ini")
    for up in (0, 1):
        for h in (0, 1):
            turned = up != h
            iota(T.row[:, 16 * up + h:16 * up + 16:2], [[1, 2], [-32 if turned and up else 32, 2], [16, 2]], (64 + 32 * up) * turned, 0, "row")
    iota(T.six[:], [[2, 6]], 0, 0, "row")
    g.wait_ge(S["nz"], 1)
    iota(T.num[:, 0:512:4], [[1, SH]], 0, 0, "num")
    for call in CALLS.split():
        write(call)
    g.wait_ge(S["sent"], sum(count.values()))

    V.memset(T.num[:], 0.0).then_inc(S["nz"], 1)
    V.memset(T.r2[:], 4.0).then_inc(S["rz"], 1)
    V.memset(T.r3[:], 4.0).then_inc(S["rz"], 1)
    V.memset(T.zero[:], 0.0).then_inc(S["rz"], 1)
    V.memset(T.rs[:], 1.0).then_inc(S["rz"], 1)
    V.wait_ge(S["ini"], 1)
    V.tensor_scalar(T.bis[:], T.ini[:], -127.0, FAR, OP.add, OP.mult).then_inc(S["bis"], 1)
    V.wait_ge(S["row"], 5)
    V.transpose(T.col[:], T.row[:]).then_inc(S["col"], 1)
    V.memset(T.tab[0:32, 0:64], 0.0).then_inc(S["pad"], 1)
    V.wait_ge(S["col"], 1)
    V.tensor_scalar(T.turn[:], T.six[:], T.col[:, 0:1], None, OP.add).then_inc(S["turn"], 1)

    def quarter(E, t):
        out, in_ = T.dq[:, 256 * (t - 1):256 * t], T.dlb[:, 256 * (t - 1):256 * t]
        E.wait_ge(S["ld%d" % min(t, 2)], 16)
        (V.tensor_scalar(out, in_, 0.25, None, OP.mult) if E is V else A.activation(out, in_, AF.Copy, scale=0.25)).then_inc(S["dq%d" % t], 1)

    def owner(step):
        if step == "u4":
            V.wait_ge(S["ldt"], 128)
            V.tensor_scalar(T.u4[:], T.ltab[:], 4.0, None, OP.mult).then_inc(S["u4"], 1)
        elif step == "bi":
            V.wait_ge(S["ldt"], 128)
            V.tensor_scalar(T.bi[:], T.ltab[:, 4:12], -FAR, None, OP.mult).then_inc(S["bi"], 1)
        elif step[0] == "d":
            quarter(V, int(step[2]))
        elif step == "vm":
            V.wait_ge(S["rs"], 9)
            V.wait_ge(S["vs"], 3)
            V.tensor_tensor_scan(T.vm[:], T.rs[:], T.vs[:], T.ini[:], OP.add, OP.min).then_inc(S["vm"], 1)
        elif step[0] == "s":
            t = step[1]
            V.wait_ge(S["rs"], 9)
            V.wait_ge(S["va" if t == "2" else "vb"], 5)
            V.tensor_tensor_scan(T["s" + t][:], T["r" + t][:], T["v" + t][:], 0.0, OP.add, OP.min).then_inc(S[step], 1)
        elif step[0] == "o":
            t = int(step[1])
            k = CH * (t - 1)
            V.wait_ge(S["s%d" % t], 1)
            V.tensor_scalar(T[step][:], T["s%d" % t][:, k:4 * k + 4:k + 1], -1.0, 508.0 + 4 * k, OP.mult, OP.add).then_inc(S[step], 1)
        elif step[0] == "m":
            t = int(step[1])
            off = "u4" if t == 1 else "o%d" % t
            hi = 256 + 256 * t
            V.wait_ge(S[off], 1)
            V.wait_ge(S["dq%d" % t], 1)
            V.wait_ge(S["g%d" % (t - 1) if t > 1 else "ldw"], 4 if t > 1 else 16)
            for e in [int(e) for e in step[2:]] or range(4):
                V.tensor_tensor(T.m[:, hi + e:hi + 256:4], T.m[:, e:hi].indirect(T[off][:, 0:4]),
                                T.dq[:, 256 * (t - 1) + e:256 * t:4], OP.add).then_inc(S["g%d" % t], 1)
        elif step[0] == "x":
            t = int(step[1])
            V.wait_ge(S["ldx%d" % (t - t % 2)], 16)
            V.quantize_mx(T.xq[:, SH * t:SH * t + SH], T.xs[:, SH * t:SH * t + SH], T.xb[:, 512 * t:512 * t + 512]).then_inc(S["qx%d" % t], 1)
        else:
            n = int(step[1])
            codes, plane, at, lo = ((T.ca, T.pa, 0, 0), (T.ca, T.pa, SH, 512), (T.cb, T.pb, 0, 768))[n - 1]
            V.wait_ge(S["g%d" % n if n > 1 else "ldw"], 4 if n > 1 else 16)
            V.quantize_mx(codes[:, at:at + SH], plane[:, at:at + SH], T.m[:, lo:lo + 512]).then_inc(S["q%d" % n], 1)

    for step in OWNER.split():
        owner(step)

    def move(E, out, in_):
        return V.tensor_copy(out, in_) if E is V else A.activation(out, in_, AF.Copy)

    def table(E, step):
        done = S["t%d" % step]
        if step == 0:
            E.wait_ge(S["pad"], 1)
            E.wait_ge(S["own"], 1)
            for who in (MATE, TWIN, DIAG):
                landed(E, "ls", who)
            for k in range(4):
                move(E, T.tab[0:32, 16 * k:16 * k + 12], T.lst[32 * k:32 * k + 32, 5:17]).then_inc(done, 1)
            return
        E.wait_ge(S["t%d" % (step - 1)], (4, 2, 1, 3)[step - 1])
        if step == 1:
            V.transpose(T.tabx[0:32, 0:64], T.tab[0:32, 0:64]).then_inc(done, 1)
            V.transpose(T.tabx[0:32, 64:96], T.tab[0:32, 0:32]).then_inc(done, 1)
        elif step == 2:
            V.transpose(T.tab[0:32, 64:128], T.tabx[0:32, 16:80]).then_inc(done, 1)
        elif step == 3:
            for k in (1, 2, 3):
                move(E, T.tab[32 * k:32 * k + 32, :], T.tab[0:32, :]).then_inc(done, 1)
        else:
            V.wait_ge(S["turn"], 1)
            V.tensor_scalar(T.tabt[:], T.tab[:].indirect(T.turn[:]), 256.0, None, OP.add).then_inc(done, 1)

    def mark(out, n, value):
        A.activation(out, T.zero[:, 0:n], AF.Identity, bias=float(value)).then_inc(S["rs"], 1)

    def compare(out, entries, bias, sem):
        A.activation(out, entries, AF.Abs, bias=bias, scale=FAR).then_inc(S[sem], 1)

    A.wait_ge(S["rz"], 4)
    mark(T.r2[:, 0:260:65], 4, LARGE)
    mark(T.r3[:, 0:516:129], 4, LARGE)
    for k in (0, 1):
        mark(T.vs[:, CH + k:198:66], 3, FAR)
    for t in (1, 2, 3):
        for k in (0, 1) if t < 3 else (0,):
            at = 66 * (t - 1) + CH + k
            mark(T.rs[:, at:at + 1], 1, (256 - (SH + CH * t - 1)) * (1 - 2 * k))
    A.wait_ge(S["num"], 1)
    A.wait_ge(S["bis"], 1)

    def lists(step):
        if step == "lr":
            A.wait_ge(S["u4"], 1)
            A.activation(T.lr[:], T.num[:].indirect(T.u4[:, 0:8]), AF.Copy).then_inc(S["lr"], 1)
        elif step == "vs":
            A.wait_ge(S["u4"], 1)
            compare(T.vs[:, 132:196], T.num[:].indirect(T.u4[:, 8:12]), T.bis[:], "vs")
            A.wait_ge(S["lr"], 1)
            for t in (1, 2):
                compare(T.vs[:, 66 * (t - 1):66 * (t - 1) + CH], T.lr[:, CH * (t - 1):CH * t], T.bis[:], "vs")
        elif step == "ba":
            A.wait_ge(S["bi"], 1)
            A.activation(T.v2[:, 0:260:65], T.bi[:, 0:4], AF.Identity, bias=508.0, scale=4 / FAR).then_inc(S["va"], 1)
        elif step == "va":
            A.wait_ge(S["bi"], 1)
            A.wait_ge(S["lr"], 1)
            for s in range(4):
                compare(T.v2[:, 65 * s + 1:65 * s + 65], T.lr[:, 0:CH], T.bi[:, s:s + 1], "va")
        elif step == "vb":
            A.wait_ge(S["bi"], 1)
            A.wait_ge(S["lr"], 1)
            A.activation(T.v3[:, 0:516:129], T.bi[:, 4:8], AF.Identity, bias=508.0, scale=4 / FAR).then_inc(S["vb"], 1)
            for s in range(4):
                compare(T.v3[:, 129 * s + 1:129 * s + 129], T.lr[:], T.bi[:, 4 + s:5 + s], "vb")
        elif step == "own":
            A.wait_ge(S["vm"], 1)
            A.activation(view("ls", OWN), T.vm[:, CH:198:66], AF.Copy, scale=-1.0).then_inc(S["own"], 1)
        else:
            quarter(A, int(step[2]))

    for step in LISTS.split():
        lists(step)

    number = {}
    seen = set()
    for n, s in enumerate(ORDER.split()):
        part, t, whos = s[0], int(s[1]), ["omtd".index(w) for w in s[2:]]
        codes, plane = (T.cb, T.pb) if part == "b" else (T.ca, T.pa)
        place = PLACE[{"a": "1", "w": "1", "d": "2", "b": "3"}[part]]
        wide = {"a": SH + CH * min(t, 2), "w": SH, "d": CH * min(t, 2), "b": CH}[part]
        lo, hi = place[whos[0]], place[whos[-1]] + wide
        short = hi - lo < SH
        if short:
            lo, hi = (hi - SH, hi) if part == "b" else (lo, lo + SH)
        for k in {"a": "12" if t else "1", "w": "1", "d": "2", "b": "3"}[part]:
            for who in [max(whos[0] - (short and part == "b"), OWN)] + whos:
                if (k, who) not in seen:
                    seen.add((k, who))
                    if who == OWN:
                        PE.wait_ge(S["q" + k], 1)
                    else:
                        landed(PE, "c" + k, who)
                        landed(PE, "p" + k, who)
        if t not in seen:
            seen.add(t)
            PE.wait_ge(S["qx%d" % t], 1)
        if n >= 8:
            PE.wait_ge(S["out%d" % (n - 8)], len(number[n - 8]))
        b = 512 * (n % 8)
        PE.matmul_mx(T.ps[:, b:b + hi - lo], T.xq[:, SH * t:SH * t + SH], T.xs[:, SH * t:SH * t + SH],
                     codes[:, lo:hi], plane[:, lo:hi], True, True).then_inc(S["made%d" % n], 1)
        number[n] = whos
        for who in whos:
            number[(part, t, who)] = (n, b + place[who] - lo, wide)

    def copy(E, part, t, first):
        n = number[(part, t, first)][0]
        E.wait_ge(S["made%d" % n], 1)
        for who in number[n]:
            _, b, k = number[(part, t, who)]
            c = {"a": 0, "w": 0, "d": SH, "b": 2 * SH}[part]
            out = T["w%d%d" % (t, who)][:, c:c + k] if t else T.yb[:, SH * ranks[who]:SH * ranks[who] + SH]
            move(E, out, T.ps[:, b:b + k]).then_inc(S["out%d" % n], 1)

    def copied(E, t, who):
        for part in "awdb":
            if (part, t, who) in number:
                n = number[(part, t, who)][0]
                E.wait_ge(S["out%d" % n], len(number[n]))

    def pick(E, t, who):
        E.wait_ge(S["t4"], 1)
        copied(E, t, who)
        k, c = 24 * who + 8 * (t - 1), 512 * t + SH * ranks[who]
        move(E, T.yb[:, c:c + SH], T["w%d%d" % (t, who)][:].indirect(T.tabt[:, k:k + 8])).then_inc(S["ga%d%d" % (t, who)], 1)

    def store(q, t, whos):
        for who in whos:
            if t:
                q.wait_ge(S["ga%d%d" % (t, who)], 1)
            else:
                copied(q, 0, who)
        c, k = 512 * t + SH * min(ranks[who] for who in whos), SH * len(whos)
        q.dma_start(T.y[:, c:c + k], T.yb[:, c:c + k]).then_inc(S["st"], 16)

    blocks = {"p": (OWN, MATE), "f": (TWIN, DIAG), "o": (OWN,), "m": (MATE,), "t": (TWIN,), "d": (DIAG,)}

    for E, todo in ((A, PLAN_A), (V, PLAN_V)):
        for s in todo.split():
            if s[0] == "t":
                table(E, int(s[1]))
            elif s[0] == "p":
                pick(E, int(s[1]), "omtd".index(s[2]))
            elif s[0] == "x":
                owner(s)
            elif s[0] == "s":
                store(A, int(s[1]), blocks[s[2]])
            else:
                copy(E, s[0], int(s[1]), "omtd".index(s[2]))

    for s in STORES.split():
        store(SY, int(s[0]), blocks[s[1]])
    SY.wait_ge(S["st"], 16 * (len(STORES.split()) + sum(s[0] == "s" for s in PLAN_A.split())))
